import numpy as np
import ml_dtypes


def mxq(x, axis, fmt="e4m3"):
    dtype, down = {"e4m3": (ml_dtypes.float8_e4m3fn, 7), "e5m2": (ml_dtypes.float8_e5m2, 14)}[fmt]
    v = np.moveaxis(np.asarray(x, np.float32).astype(ml_dtypes.bfloat16).astype(np.float64), axis, -1)
    blocks = v.reshape(v.shape[:-1] + (-1, 32))
    amax = np.abs(blocks).max(-1, keepdims=True)
    byte = np.maximum(np.where(amax > 0, np.frexp(amax)[1] - 1 + 127, 0) - down, 1)
    scale = np.exp2(byte - 127.0)
    codes = (blocks / scale).astype(np.float32).astype(dtype).astype(np.float64)
    return np.moveaxis((codes * scale).reshape(v.shape), -1, axis)


WIDE = False


def mx_kscale(k):
    if not WIDE:
        return np.ones(k)
    levels = np.array([10, -10, 5, -5, 0])
    if k % 512:
        return np.exp2(np.random.permutation(np.resize(levels, k // 32))).repeat(32)
    a = np.empty((k // 512, 16))
    for p in range(k // 512):
        a[p, :8] = np.random.permutation(np.resize(levels, 8))
        for g in range(8):
            far = levels[np.abs(levels - a[p, g]) >= 10]
            a[p, g + 8] = far[np.random.randint(len(far))]
    return np.exp2(a.ravel()).repeat(32)


def f64(x):
    return np.asarray(x).astype(np.float64)


def striped(idx):
    return np.tile(idx.reshape(-1, 16).T, (8, 1)).astype(np.uint16)


def unstriped(offs):
    return offs[:16].T.reshape(-1).astype(np.int64)


E2M1 = np.array([0.0, 0.5, 1.0, 1.5, 2.0, 3.0, 4.0, 6.0, -0.0, -0.5, -1.0, -1.5, -2.0, -3.0, -4.0, -6.0])


def pack_weight(w, fmt):
    k, n = w.shape
    w = f64(np.asarray(w, np.float32).astype(ml_dtypes.bfloat16)).reshape(k // 32, 32, n)
    amax = np.abs(w).max(1)
    if fmt == "e4m3":
        byte = np.frexp(amax)[1] - 1 + 127 - 7
    else:
        mant, ex = np.frexp(amax / 6.0)
        byte = np.where(mant > 0.5, ex, ex - 1) + 127
    byte = np.clip(np.where(amax > 0, byte, 1), 1, 254)
    scaled = (w * np.exp2(127.0 - byte)[:, None, :]).reshape(k, n).astype(np.float32)
    by_word = np.ascontiguousarray(scaled.reshape(k // 512, 128, 4, n).transpose(0, 1, 3, 2))
    if fmt == "e4m3":
        words = by_word.astype(ml_dtypes.float8_e4m3fn).view(np.uint8)
    else:
        c = by_word.astype(ml_dtypes.float4_e2m1fn).view(np.uint8) & 0xF
        words = (c[..., 0::2] | (c[..., 1::2] << 4)).reshape(k // 512, 128, 2 * n)
    return np.ascontiguousarray(words), np.ascontiguousarray(byte.astype(np.uint8).reshape(k // 512, 16, n))


def unpack_weight(words, scales, fmt):
    g, _, n = scales.shape
    words = np.ascontiguousarray(words).reshape(g, 128, n, -1)
    if fmt == "e4m3":
        vals = words.view(ml_dtypes.float8_e4m3fn).astype(np.float64)
    else:
        nib = np.empty((g, 128, n, 4), np.uint8)
        nib[..., 0::2] = words & 0xF
        nib[..., 1::2] = words >> 4
        vals = E2M1[nib]
    vals = vals * np.repeat(np.exp2(scales.astype(np.float64) - 127.0), 8, axis=1)[..., None]
    return vals.transpose(0, 1, 3, 2).reshape(g * 512, n)


def relu(v):
    return np.maximum(v, 0.0)


K, T, E, H, N = 512, 768, 4, 512, 384
COUNTS = (256, 384, 512, 384)
STARTS = np.cumsum((0,) + COUNTS)


def by_expert(wq, xq):
    return np.concatenate([wq[e].T @ xq[:, STARTS[e]:STARTS[e + 1]] for e in range(E)], axis=1)


def setup_inputs():
    n = np.random.standard_normal
    s = mx_kscale(K)[:, None]
    u = mx_kscale(H)
    both = np.repeat(np.arange(E), COUNTS)
    pair = np.stack([both[:T], both[T:]])[:, np.random.permutation(T)]
    pair = np.where(np.random.rand(T) < 0.5, pair, pair[::-1])
    order = np.argsort(pair.reshape(-1), kind="stable")
    slot_token = order % T; pos = np.empty(2 * T, np.int64); pos[order] = np.arange(2 * T); pos = pos.reshape(2, T)
    g = np.random.uniform(0.2, 0.8, T)
    w1 = [pack_weight(m, "e2m1") for m in n((E, K, H)) / np.sqrt(K) / s[None] * u[None, None, :]]
    w2 = [pack_weight(m, "e2m1") for m in n((E, H, N)) / np.sqrt(H) / u[None, :, None]]
    return {
        "xT": (n((K, T)) * s).astype(np.float32),
        "w1_words": np.stack([m[0] for m in w1]),
        "w1_scales": np.stack([m[1] for m in w1]),
        "w2_words": np.stack([m[0] for m in w2]),
        "w2_scales": np.stack([m[1] for m in w2]),
        "gate": np.stack([np.tile(g, (N, 1)), np.tile(1.0 - g, (N, 1))]).astype(np.float32),
        "offs": striped(slot_token),
        "pos1": striped(pos[0]),
        "pos2": striped(pos[1]),
    }


def reference(xT, w1_words, w1_scales, w2_words, w2_scales, gate, offs, pos1, pos2):
    idx = unstriped(offs)
    w1 = np.stack([unpack_weight(w1_words[e], w1_scales[e], "e2m1") for e in range(E)])
    w2 = np.stack([unpack_weight(w2_words[e], w2_scales[e], "e2m1") for e in range(E)])
    xq = mxq(f64(xT)[:, idx], 0, "e4m3")
    h = relu(by_expert(w1, xq))
    y = by_expert(w2, mxq(h, 0, "e4m3"))
    return f64(gate[0]) * y[:, unstriped(pos1)] + f64(gate[1]) * y[:, unstriped(pos2)]

@@ -1,0 +1,249 @@
+from contextlib import ExitStack
+
+import concourse.mybir as mybir
+
+K, T, E, H, N = 512, 768, 4, 512, 384
+COUNTS = (256, 384, 512, 384)
+STARTS = (0, 256, 640, 1152)
+S = 1536
+P = 128
+PACK = 4
+CH = 128
+XC = 256
+FLOPS = 2 * S * (K * H + H * N)
+
+F32 = mybir.dt.float32
+BF16 = mybir.dt.bfloat16
+I32 = mybir.dt.int32
+U32 = mybir.dt.uint32
+U16 = mybir.dt.uint16
+U8 = mybir.dt.uint8
+FP8X4 = mybir.dt.float8_e4m3fn_x4
+FP4X4 = mybir.dt.float4_e2m1fn_x4
+COPY = mybir.ActivationFunctionType.Copy
+RELU = mybir.ActivationFunctionType.Relu
+MULT = mybir.AluOpType.mult
+ADD = mybir.AluOpType.add
+
+
+def tile_moe_rag_mlp_relu_kernel(
+    tc, xT, w1_words, w1_scales, w2_words, w2_scales, gate, offs, pos1, pos2, out
+):
+    nc = tc.nc
+    with ExitStack() as ctx:
+        lists = ctx.enter_context(tc.tile_pool(name="lists", bufs=1))
+        keep = ctx.enter_context(tc.tile_pool(name="keep", bufs=1))
+        ring = ctx.enter_context(tc.tile_pool(name="ring", bufs=3))
+        psum = ctx.enter_context(tc.psum_pool(name="psum", bufs=1))
+
+        offs_t = lists.tile([P, 2 * T // 16], U16, name="offs_t")
+        pos1_t = lists.tile([P, T // 16], U16, name="pos1_t")
+        pos2_t = lists.tile([P, T // 16], U16, name="pos2_t")
+
+        w1_raw = keep.tile([P, E, 2 * H], U8, name="w1_raw", align_bytes=64)
+        w1_codes = keep.tile([P, E, 2 * H], U8, name="w1_codes", align_bytes=64)
+        w1s_raw = keep.tile([P, E, H], U8, name="w1s_raw", align_bytes=64)
+        w1s = keep.tile([P, E, H], U8, name="w1s", align_bytes=64)
+        w2_codes = keep.tile([P, E, 2 * N], U8, name="w2_codes", align_bytes=64)
+        w2s = keep.tile([P, E, N], U8, name="w2s", align_bytes=64)
+        x_raw = [keep.tile([P, PACK, XC], F32, name=f"x_raw{c}", align_bytes=64) for c in range(3)]
+        x_grp = [keep.tile([P, XC, PACK], BF16, name=f"x_grp{c}", align_bytes=64) for c in range(3)]
+        x_codes = keep.tile([P, T], U32, name="x_codes", align_bytes=64)
+        x_scales = keep.tile([P, T], U8, name="x_scales", align_bytes=64)
+        gates = [keep.tile([P, 2, T], F32, name=f"gates{b}", align_bytes=64) for b in range(3)]
+        ys = [keep.tile([P, S], F32, name=f"y{b}", align_bytes=64) for b in range(3)]
+
+        nc.gpsimd.memset(w1s_raw[:].rearrange("p e n -> p (e n)").bitcast(I32), 0)
+        nc.gpsimd.memset(x_scales[:], 0)
+        nc.gpsimd.memset(w2s[:].rearrange("p e n -> p (e n)").bitcast(I32), 0)
+
+        def load_x(c):
+            nc.sync.dma_start(out=x_raw[c][:], in_=xT[:, c * XC : (c + 1) * XC].rearrange("(p j) w -> p j w", j=PACK))
+
+        def load_w1(i):
+            nc.sync.dma_start(
+                out=w1_raw[:, 2 * i : 2 * i + 2, :].bitcast(I32),
+                in_=w1_words[2 * i : 2 * i + 2, 0].rearrange("e p b -> p e b").bitcast(I32),
+            )
+
+        for q in range(4):
+            nc.scalar.dma_start(
+                out=w1s_raw[32 * q : 32 * q + 4].bitcast(I32),
+                in_=w1_scales[:, 0, 4 * q : 4 * q + 4, :].rearrange("e q n -> q e n").bitcast(I32),
+            )
+        load_w1(0)
+        load_x(0)
+        load_w1(1)
+        load_x(1)
+        load_x(2)
+        nc.sync.dma_start(offs_t[:], offs)
+        nc.sync.dma_start(out=w2_codes[:].bitcast(I32), in_=w2_words[:, 0].rearrange("e p b -> p e b").bitcast(I32))
+        for q in range(4):
+            nc.sync.dma_start(
+                out=w2s[32 * q : 32 * q + 4].bitcast(I32),
+                in_=w2_scales[:, 0, 4 * q : 4 * q + 4, :].rearrange("e q n -> q e n").bitcast(I32),
+            )
+        nc.sync.dma_start(pos1_t[:], pos1)
+        nc.sync.dma_start(pos2_t[:], pos2)
+        for b in range(3):
+            nc.sync.dma_start(out=gates[b][:], in_=gate[:, b * P : (b + 1) * P, :].rearrange("g p t -> p g t"))
+
+        def x_quant(c):
+            nc.vector.quantize_mx(
+                out=x_codes[:, c * XC : (c + 1) * XC].bitcast(FP8X4),
+                scales=x_scales[:, c * XC : (c + 1) * XC],
+                in_=x_grp[c][:].rearrange("p w j -> p (w j)"),
+            )
+
+        def interleave(engine, c, lo, hi):
+            o = x_grp[c][:, lo:hi, :].rearrange("p (c i) t -> p c t i", i=4)
+            i = x_raw[c][:, :, lo:hi].rearrange("p t (c i) -> p c t i", i=4)
+            if engine == "S":
+                nc.scalar.activation(o, i, COPY)
+            else:
+                nc.vector.tensor_copy(o, i)
+
+        def w1_permute(i):
+            es = slice(2 * i, 2 * i + 2)
+            nc.vector.tensor_copy(
+                out=w1_codes[:, es, :].bitcast(U16).rearrange("p e (t m) -> p e t m", t=PACK),
+                in_=w1_raw[:, es, :].bitcast(U16).rearrange("p e (m t) -> p e t m", t=PACK),
+            )
+            nc.vector.tensor_copy(
+                out=w1s[:, es, :].rearrange("p e (t m) -> p e t m", t=PACK),
+                in_=w1s_raw[:, es, :].rearrange("p e (m t) -> p e t m", t=PACK),
+            )
+
+        interleave("S", 0, 0, XC)
+        w1_permute(0)
+        w1_permute(1)
+        x_quant(0)
+        interleave("S", 1, 0, 160)
+        interleave("V", 1, 160, XC)
+        interleave("V", 2, 0, 160)
+        x_quant(1)
+        interleave("S", 2, 160, XC)
+        x_quant(2)
+
+        xg = []
+        xgs = []
+        for e in range(E):
+            words = keep.tile([P, COUNTS[e]], U32, name=f"xg{e}", align_bytes=64)
+            bytes_ = keep.tile([P, COUNTS[e]], U8, name=f"xgs{e}", align_bytes=64)
+            step = 256 if e == 2 else COUNTS[e]
+            for lo in range(0, COUNTS[e], step):
+                cols = slice((STARTS[e] + lo) // 16, (STARTS[e] + lo + step) // 16)
+                nc.vector.tensor_copy(words[:, lo : lo + step], x_codes[:].indirect(offs_t[:, cols]))
+                nc.vector.tensor_copy(bytes_[:, lo : lo + step], x_scales[:].indirect(offs_t[:, cols]))
+            xg.append(words)
+            xgs.append(bytes_)
+
+        chunks = [(e, s) for e in range(E) for s in range(0, COUNTS[e], CH)]
+        vector_chunks = (7, 9, 11)
+
+        def layer1(c, h_grp, at):
+            e, s = chunks[c]
+            acc = psum.tile([P, PACK, CH], F32, name="acc", bufs=5)
+            for t in range(PACK):
+                nc.tensor.matmul_mx(
+                    out=acc[:, t, :],
+                    lhsT=w1_codes[:, e, 256 * t : 256 * t + 256].bitcast(FP4X4),
+                    lhsT_scale=w1s[:, e, 128 * t : 128 * t + 128],
+                    rhs=xg[e][:, s : s + CH].bitcast(FP8X4),
+                    rhs_scale=xgs[e][:, s : s + CH],
+                    start=True,
+                    stop=True,
+                )
+            o = h_grp[:, at : at + CH, :]
+            a = acc[:].rearrange("p t n -> p n t")
+            if c in vector_chunks:
+                nc.vector.tensor_scalar_max(o, a, 0.0)
+            else:
+                nc.scalar.activation(o, a, RELU)
+
+        groups = [(0, 1), (2, 3), (4,), (5, 6), (7,), (8,), (9,), (10,), (11,)]
+        h_grps, h_codes, h_scales = {}, {}, {}
+
+        def h_make(g):
+            h_grps[g] = keep.tile([P, CH * len(g), PACK], BF16, name=f"h_grp{g[0]}", align_bytes=64)
+            for n, c in enumerate(g):
+                layer1(c, h_grps[g], n * CH)
+
+        def h_quant(g):
+            h_codes[g] = keep.tile([P, CH * len(g)], U32, name=f"h_codes{g[0]}", align_bytes=64)
+            h_scales[g] = keep.tile([P, CH * len(g)], U8, name=f"h_scales{g[0]}", align_bytes=64)
+            nc.vector.quantize_mx(
+                out=h_codes[g][:].bitcast(FP8X4),
+                scales=h_scales[g][:],
+                in_=h_grps[g][:].rearrange("p n t -> p (n t)"),
+            )
+
+        for g in groups[:6]:
+            h_make(g)
+        for g in groups[:3]:
+            h_quant(g)
+        for g in groups[6:8]:
+            h_make(g)
+        for g in groups[3:5]:
+            h_quant(g)
+        h_make(groups[8])
+        for g in groups[5:]:
+            h_quant(g)
+
+        def layer2(b, g, yp):
+            e = chunks[g[0]][0]
+            k, at = g[0] // 4, g[0] % 4 * CH
+            nc.tensor.matmul_mx(
+                out=yp[k][:, at : at + CH * len(g)],
+                lhsT=w2_codes[:, e, 256 * b : 256 * b + 256].bitcast(FP4X4),
+                lhsT_scale=w2s[:, e, 128 * b : 128 * b + 128],
+                rhs=h_codes[g][:].bitcast(FP8X4),
+                rhs_scale=h_scales[g][:],
+                start=True,
+                stop=True,
+            )
+
+        y0 = [psum.tile([P, 512], F32, name=f"yp{k}", bufs=1) for k in range(3)]
+        for g in groups:
+            layer2(0, g, y0)
+            if g == (3,) or g == (2, 3):
+                nc.scalar.activation(ys[0][:, 0:512], y0[0][:], COPY)
+            elif g == (7,):
+                nc.scalar.activation(ys[0][:, 512:1024], y0[1][:], COPY)
+            elif g == (10,):
+                nc.scalar.activation(ys[0][:, 1024:1408], y0[2][:, 0:384], COPY)
+            elif g == (11,):
+                nc.vector.tensor_copy(ys[0][:, 1408:1536], y0[2][:, 384:512])
+
+        for b in (1, 2):
+            yb = [psum.tile([P, 512], F32, name=f"yp{k}", bufs=1) for k in range(3)]
+            for g in groups:
+                layer2(b, g, yb)
+            for k in range(3):
+                nc.scalar.activation(ys[b][:, 512 * k : 512 * k + 512], yb[k][:], COPY)
+
+        def mul(b, r, lo, hi):
+            g = ring.tile([P, T], F32, name=f"m{r}", bufs=4, align_bytes=64)
+            pos = (pos1_t, pos2_t)[r]
+            nc.vector.tensor_tensor(
+                g[:, lo:hi], ys[b][:].indirect(pos[:, lo // 16 : hi // 16]), gates[b][:, r, lo:hi], MULT
+            )
+            return g
+
+        def finish(b, m1, m2, lo, hi):
+            o = ring.tile([P, T], F32, name="o", bufs=5, align_bytes=64)
+            nc.vector.tensor_tensor(o[:, lo:hi], m1[:, lo:hi], m2[:, lo:hi], ADD)
+            nc.sync.dma_start(out=out[b * P : (b + 1) * P, lo:hi], in_=o[:, lo:hi])
+
+        parts = [(0, 0, T), (1, 0, T), (2, 0, 384), (2, 384, 576), (2, 576, T)]
+        pending = None
+        for b, lo, hi in parts:
+            m1 = mul(b, 0, lo, hi)
+            if pending is not None and hi < T or b < 2 and pending is not None:
+                finish(*pending)
+                pending = None
+            m2 = mul(b, 1, lo, hi)
+            if pending is not None:
+                finish(*pending)
+            pending = (b, m1, m2, lo, hi)
+        finish(*pending)

@@ -9,7 +9,8 @@ S = 1536
 P = 128
 PACK = 4
 CH = 128
-XC = 256
+XW = (128, 256, 256, 128)
+X0 = (0, 128, 384, 640)
 FLOPS = 2 * S * (K * H + H * N)
 
 F32 = mybir.dt.float32
@@ -42,15 +43,14 @@ def tile_moe_rag_mlp_relu_kernel(
 
         w1_raw = keep.tile([P, E, 2 * H], U8, name="w1_raw", align_bytes=64)
         w1_codes = keep.tile([P, E, 2 * H], U8, name="w1_codes", align_bytes=64)
-        w1s_raw = keep.tile([P, E, H], U8, name="w1s_raw", align_bytes=64)
+        w1s_raw = keep.tile([P, E, H], U8, name="shared", align_bytes=64)
         w1s = keep.tile([P, E, H], U8, name="w1s", align_bytes=64)
         w2_codes = keep.tile([P, E, 2 * N], U8, name="w2_codes", align_bytes=64)
         w2s = keep.tile([P, E, N], U8, name="w2s", align_bytes=64)
-        x_raw = [keep.tile([P, PACK, XC], F32, name=f"x_raw{c}", align_bytes=64) for c in range(3)]
-        x_grp = [keep.tile([P, XC, PACK], BF16, name=f"x_grp{c}", align_bytes=64) for c in range(3)]
+        x_raw = [keep.tile([P, PACK, w], F32, name=f"x_raw{c}", align_bytes=64) for c, w in enumerate(XW)]
         x_codes = keep.tile([P, T], U32, name="x_codes", align_bytes=64)
         x_scales = keep.tile([P, T], U8, name="x_scales", align_bytes=64)
-        gates = [keep.tile([P, 2, T], F32, name=f"gates{b}", align_bytes=64) for b in range(3)]
+        gates = keep.tile([P, 2, T], F32, name="gates", align_bytes=64)
         ys = [keep.tile([P, S], F32, name=f"y{b}", align_bytes=64) for b in range(3)]
 
         nc.gpsimd.memset(w1s_raw[:].rearrange("p e n -> p (e n)").bitcast(I32), 0)
@@ -58,7 +58,7 @@ def tile_moe_rag_mlp_relu_kernel(
         nc.gpsimd.memset(w2s[:].rearrange("p e n -> p (e n)").bitcast(I32), 0)
 
         def load_x(c):
-            nc.sync.dma_start(out=x_raw[c][:], in_=xT[:, c * XC : (c + 1) * XC].rearrange("(p j) w -> p j w", j=PACK))
+            nc.sync.dma_start(out=x_raw[c][:], in_=xT[:, X0[c] : X0[c] + XW[c]].rearrange("(p j) w -> p j w", j=PACK))
 
         def load_w1(i):
             nc.sync.dma_start(
@@ -72,10 +72,11 @@ def tile_moe_rag_mlp_relu_kernel(
                 in_=w1_scales[:, 0, 4 * q : 4 * q + 4, :].rearrange("e q n -> q e n").bitcast(I32),
             )
         load_w1(0)
-        load_x(0)
         load_w1(1)
+        load_x(0)
         load_x(1)
         load_x(2)
+        load_x(3)
         nc.sync.dma_start(offs_t[:], offs)
         nc.sync.dma_start(out=w2_codes[:].bitcast(I32), in_=w2_words[:, 0].rearrange("e p b -> p e b").bitcast(I32))
         for q in range(4):
@@ -85,13 +86,12 @@ def tile_moe_rag_mlp_relu_kernel(
             )
         nc.sync.dma_start(pos1_t[:], pos1)
         nc.sync.dma_start(pos2_t[:], pos2)
-        for b in range(3):
-            nc.sync.dma_start(out=gates[b][:], in_=gate[:, b * P : (b + 1) * P, :].rearrange("g p t -> p g t"))
+        nc.sync.dma_start(out=gates[:], in_=gate[:, 0:P, :].rearrange("g p t -> p g t"))
 
         def x_quant(c):
             nc.vector.quantize_mx(
-                out=x_codes[:, c * XC : (c + 1) * XC].bitcast(FP8X4),
-                scales=x_scales[:, c * XC : (c + 1) * XC],
+                out=x_codes[:, X0[c] : X0[c] + XW[c]].bitcast(FP8X4),
+                scales=x_scales[:, X0[c] : X0[c] + XW[c]],
                 in_=x_grp[c][:].rearrange("p w j -> p (w j)"),
             )
 
@@ -114,119 +114,110 @@ def tile_moe_rag_mlp_relu_kernel(
                 in_=w1s_raw[:, es, :].rearrange("p e (m t) -> p e t m", t=PACK),
             )
 
-        interleave("S", 0, 0, XC)
         w1_permute(0)
         w1_permute(1)
-        x_quant(0)
-        interleave("S", 1, 0, 160)
-        interleave("V", 1, 160, XC)
-        interleave("V", 2, 0, 160)
-        x_quant(1)
-        interleave("S", 2, 160, XC)
-        x_quant(2)
-
-        xg = []
-        xgs = []
-        for e in range(E):
-            words = keep.tile([P, COUNTS[e]], U32, name=f"xg{e}", align_bytes=64)
-            bytes_ = keep.tile([P, COUNTS[e]], U8, name=f"xgs{e}", align_bytes=64)
-            step = 256 if e == 2 else COUNTS[e]
-            for lo in range(0, COUNTS[e], step):
-                cols = slice((STARTS[e] + lo) // 16, (STARTS[e] + lo + step) // 16)
-                nc.vector.tensor_copy(words[:, lo : lo + step], x_codes[:].indirect(offs_t[:, cols]))
-                nc.vector.tensor_copy(bytes_[:, lo : lo + step], x_scales[:].indirect(offs_t[:, cols]))
-            xg.append(words)
-            xgs.append(bytes_)
+        x_grp = [
+            keep.tile([P, w, PACK], BF16, name="shared" if c == 1 else f"x_grp{c}", align_bytes=64)
+            for c, w in enumerate(XW)
+        ]
+        interleave("S", 0, 0, 128)
+        for c in (1, 2, 3):
+            cut = XW[c] * 5 // 8
+            interleave("V", c, 0, cut)
+            interleave("S", c, cut, XW[c])
+            x_quant(c - 1)
+        x_quant(3)
 
         chunks = [(e, s) for e in range(E) for s in range(0, COUNTS[e], CH)]
-        vector_chunks = (7, 9, 11)
+        groups = [(0, 4), (4, 8), (8, 10), (10, 11), (11, 12)]
+        vector_chunks = ()
+        pieces = [(c, c + 1) for c in range(12)]
 
-        def layer1(c, h_grp, at):
-            e, s = chunks[c]
-            acc = psum.tile([P, PACK, CH], F32, name="acc", bufs=5)
-            for t in range(PACK):
-                nc.tensor.matmul_mx(
-                    out=acc[:, t, :],
-                    lhsT=w1_codes[:, e, 256 * t : 256 * t + 256].bitcast(FP4X4),
-                    lhsT_scale=w1s[:, e, 128 * t : 128 * t + 128],
-                    rhs=xg[e][:, s : s + CH].bitcast(FP8X4),
-                    rhs_scale=xgs[e][:, s : s + CH],
-                    start=True,
-                    stop=True,
-                )
-            o = h_grp[:, at : at + CH, :]
-            a = acc[:].rearrange("p t n -> p n t")
-            if c in vector_chunks:
-                nc.vector.tensor_scalar_max(o, a, 0.0)
-            else:
-                nc.scalar.activation(o, a, RELU)
+        def bank(k):
+            return psum.tile([P, PACK, CH], F32, name=f"bank{k}", bufs=1)
 
-        groups = [(0, 1), (2, 3), (4,), (5, 6), (7,), (8,), (9,), (10,), (11,)]
-        h_grps, h_codes, h_scales = {}, {}, {}
+        xg, xgs = {}, {}
+        for lo, hi in pieces:
+            words = keep.tile([P, (hi - lo) * CH], U32, name=f"xg{lo}", align_bytes=64)
+            bytes_ = keep.tile([P, (hi - lo) * CH], U8, name=f"xgs{lo}", align_bytes=64)
+            cols = slice(lo * CH // 16, hi * CH // 16)
+            nc.vector.tensor_copy(words[:], x_codes[:].indirect(offs_t[:, cols]))
+            nc.vector.tensor_copy(bytes_[:], x_scales[:].indirect(offs_t[:, cols]))
+            for c in range(lo, hi):
+                xg[c] = words[:, (c - lo) * CH : (c - lo + 1) * CH]
+                xgs[c] = bytes_[:, (c - lo) * CH : (c - lo + 1) * CH]
 
-        def h_make(g):
-            h_grps[g] = keep.tile([P, CH * len(g), PACK], BF16, name=f"h_grp{g[0]}", align_bytes=64)
-            for n, c in enumerate(g):
-                layer1(c, h_grps[g], n * CH)
+        h_grp = {}
+        for lo, hi in groups:
+            h_grp[lo] = keep.tile([P, (hi - lo) * CH, PACK], BF16, name=f"h_grp{lo}", align_bytes=64)
+            for c in range(lo, hi):
+                e = chunks[c][0]
+                acc = bank(c % 8)
+                for t in range(PACK):
+                    nc.tensor.matmul_mx(
+                        out=acc[:, t, :],
+                        lhsT=w1_codes[:, e, 256 * t : 256 * t + 256].bitcast(FP4X4),
+                        lhsT_scale=w1s[:, e, 128 * t : 128 * t + 128],
+                        rhs=xg[c].bitcast(FP8X4),
+                        rhs_scale=xgs[c],
+                        start=True,
+                        stop=True,
+                    )
+                o = h_grp[lo][:, (c - lo) * CH : (c - lo + 1) * CH, :]
+                a = acc[:].rearrange("p t n -> p n t")
+                if c in vector_chunks:
+                    nc.vector.tensor_scalar_max(o, a, 0.0)
+                else:
+                    nc.scalar.activation(o, a, RELU)
 
-        def h_quant(g):
-            h_codes[g] = keep.tile([P, CH * len(g)], U32, name=f"h_codes{g[0]}", align_bytes=64)
-            h_scales[g] = keep.tile([P, CH * len(g)], U8, name=f"h_scales{g[0]}", align_bytes=64)
+        h_codes, h_scales = {}, {}
+        for lo, hi in groups:
+            h_codes[lo] = keep.tile([P, (hi - lo) * CH], U32, name=f"h_codes{lo}", align_bytes=64)
+            h_scales[lo] = keep.tile([P, (hi - lo) * CH], U8, name=f"h_scales{lo}", align_bytes=64)
             nc.vector.quantize_mx(
-                out=h_codes[g][:].bitcast(FP8X4),
-                scales=h_scales[g][:],
-                in_=h_grps[g][:].rearrange("p n t -> p (n t)"),
+                out=h_codes[lo][:].bitcast(FP8X4),
+                scales=h_scales[lo][:],
+                in_=h_grp[lo][:].rearrange("p n t -> p (n t)"),
             )
 
-        for g in groups[:6]:
-            h_make(g)
-        for g in groups[:3]:
-            h_quant(g)
-        for g in groups[6:8]:
-            h_make(g)
-        for g in groups[3:5]:
-            h_quant(g)
-        h_make(groups[8])
-        for g in groups[5:]:
-            h_quant(g)
+        runs = [(0, 2), (2, 4), (4, 5), (5, 7), (7, 8), (8, 9), (9, 10), (10, 11), (11, 12)]
 
-        def layer2(b, g, yp):
-            e = chunks[g[0]][0]
-            k, at = g[0] // 4, g[0] % 4 * CH
-            nc.tensor.matmul_mx(
-                out=yp[k][:, at : at + CH * len(g)],
-                lhsT=w2_codes[:, e, 256 * b : 256 * b + 256].bitcast(FP4X4),
-                lhsT_scale=w2s[:, e, 128 * b : 128 * b + 128],
-                rhs=h_codes[g][:].bitcast(FP8X4),
-                rhs_scale=h_scales[g][:],
-                start=True,
-                stop=True,
-            )
+        def layer2(b, k, first, last, engine):
+            yp = bank(k)
+            flat = yp[:].rearrange("p t n -> p (t n)")
+            for lo, hi in runs:
+                if first <= lo < last:
+                    e = chunks[lo][0]
+                    g = max(g for g, g_end in groups if g <= lo)
+                    cols = slice((lo - g) * CH, (hi - g) * CH)
+                    nc.tensor.matmul_mx(
+                        out=flat[:, (lo - first) * CH : (hi - first) * CH],
+                        lhsT=w2_codes[:, e, 256 * b : 256 * b + 256].bitcast(FP4X4),
+                        lhsT_scale=w2s[:, e, 128 * b : 128 * b + 128],
+                        rhs=h_codes[g][:, cols].bitcast(FP8X4),
+                        rhs_scale=h_scales[g][:, cols],
+                        start=True,
+                        stop=True,
+                    )
+            o, i = ys[b][:, first * CH : last * CH], flat[:, 0 : (last - first) * CH]
+            if engine == "S":
+                nc.scalar.activation(o, i, COPY)
+            else:
+                nc.vector.tensor_copy(o, i)
 
-        y0 = [psum.tile([P, 512], F32, name=f"yp{k}", bufs=1) for k in range(3)]
-        for g in groups:
-            layer2(0, g, y0)
-            if g == (3,) or g == (2, 3):
-                nc.scalar.activation(ys[0][:, 0:512], y0[0][:], COPY)
-            elif g == (7,):
-                nc.scalar.activation(ys[0][:, 512:1024], y0[1][:], COPY)
-            elif g == (10,):
-                nc.scalar.activation(ys[0][:, 1024:1408], y0[2][:, 0:384], COPY)
-            elif g == (11,):
-                nc.vector.tensor_copy(ys[0][:, 1408:1536], y0[2][:, 384:512])
-
+        layer2(0, 4, 0, 4, "S")
+        layer2(0, 5, 4, 8, "S")
+        layer2(0, 6, 8, 10, "S")
+        layer2(0, 7, 10, 12, "V")
         for b in (1, 2):
-            yb = [psum.tile([P, 512], F32, name=f"yp{k}", bufs=1) for k in range(3)]
-            for g in groups:
-                layer2(b, g, yb)
             for k in range(3):
-                nc.scalar.activation(ys[b][:, 512 * k : 512 * k + 512], yb[k][:], COPY)
+                layer2(b, 4 + k, 4 * k, 4 * k + 4, "S")
 
         def mul(b, r, lo, hi):
             g = ring.tile([P, T], F32, name=f"m{r}", bufs=4, align_bytes=64)
             pos = (pos1_t, pos2_t)[r]
             nc.vector.tensor_tensor(
-                g[:, lo:hi], ys[b][:].indirect(pos[:, lo // 16 : hi // 16]), gates[b][:, r, lo:hi], MULT
+                g[:, lo:hi], ys[b][:].indirect(pos[:, lo // 16 : hi // 16]), gates[:, r, lo:hi], MULT
             )
             return g
 

@@ -129,9 +129,9 @@ def tile_moe_rag_mlp_relu_kernel(
         x_quant(3)
 
         chunks = [(e, s) for e in range(E) for s in range(0, COUNTS[e], CH)]
-        groups = [(0, 4), (4, 8), (8, 10), (10, 11), (11, 12)]
-        vector_chunks = ()
-        pieces = [(c, c + 1) for c in range(12)]
+        groups = [(0, 4), (4, 8), (8, 10), (10, 12)]
+        vector_chunks = (11,)
+        pieces = [(0, 1), (1, 2), (2, 4), (4, 6), (6, 9), (9, 12)]
 
         def bank(k):
             return psum.tile([P, PACK, CH], F32, name=f"bank{k}", bufs=1)
@@ -180,7 +180,7 @@ def tile_moe_rag_mlp_relu_kernel(
                 in_=h_grp[lo][:].rearrange("p n t -> p (n t)"),
             )
 
-        runs = [(0, 2), (2, 4), (4, 5), (5, 7), (7, 8), (8, 9), (9, 10), (10, 11), (11, 12)]
+        runs = [(0, 2), (2, 4), (4, 5), (5, 7), (7, 8), (8, 9), (9, 10), (10, 12)]
 
         def layer2(b, k, first, last, engine):
             yp = bank(k)

@@ -54,7 +54,7 @@ def tile_moe_rag_mlp_relu_kernel(
         ys = [keep.tile([P, S], F32, name=f"y{b}", align_bytes=64) for b in range(3)]
 
         nc.gpsimd.memset(w1s_raw[:].rearrange("p e n -> p (e n)").bitcast(I32), 0)
-        nc.gpsimd.memset(x_scales[:], 0)
+        nc.gpsimd.memset(x_scales[:].bitcast(I32), 0)
         nc.gpsimd.memset(w2s[:].rearrange("p e n -> p (e n)").bitcast(I32), 0)
 
         def load_x(c):
@@ -67,7 +67,7 @@ def tile_moe_rag_mlp_relu_kernel(
             )
 
         for q in range(4):
-            nc.scalar.dma_start(
+            nc.sync.dma_start(
                 out=w1s_raw[32 * q : 32 * q + 4].bitcast(I32),
                 in_=w1_scales[:, 0, 4 * q : 4 * q + 4, :].rearrange("e q n -> q e n").bitcast(I32),
             )
@@ -207,7 +207,7 @@ def tile_moe_rag_mlp_relu_kernel(
 
         layer2(0, 4, 0, 4, "S")
         layer2(0, 5, 4, 8, "S")
-        layer2(0, 6, 8, 10, "S")
+        layer2(0, 2, 8, 10, "V")
         layer2(0, 7, 10, 12, "V")
         for b in (1, 2):
             for k in range(3):

@@ -1,6 +1,7 @@
 from contextlib import ExitStack
 
 import concourse.mybir as mybir
+from concourse.masks import make_identity
 
 K, T, E, H, N = 512, 768, 4, 512, 384
 COUNTS = (256, 384, 512, 384)
@@ -34,7 +35,6 @@ def tile_moe_rag_mlp_relu_kernel(
     with ExitStack() as ctx:
         lists = ctx.enter_context(tc.tile_pool(name="lists", bufs=1))
         keep = ctx.enter_context(tc.tile_pool(name="keep", bufs=1))
-        ring = ctx.enter_context(tc.tile_pool(name="ring", bufs=3))
         psum = ctx.enter_context(tc.psum_pool(name="psum", bufs=1))
 
         offs_t = lists.tile([P, 2 * T // 16], U16, name="offs_t")
@@ -48,14 +48,15 @@ def tile_moe_rag_mlp_relu_kernel(
         w2_codes = keep.tile([P, E, 2 * N], U8, name="w2_codes", align_bytes=64)
         w2s = keep.tile([P, E, N], U8, name="w2s", align_bytes=64)
         x_raw = [keep.tile([P, PACK, w], F32, name=f"x_raw{c}", align_bytes=64) for c, w in enumerate(XW)]
-        x_codes = keep.tile([P, T], U32, name="x_codes", align_bytes=64)
         x_scales = keep.tile([P, T], U8, name="x_scales", align_bytes=64)
         gates = keep.tile([P, 2, T], F32, name="gates", align_bytes=64)
+        ident = keep.tile([P, P], F32, name="ident", align_bytes=64)
         ys = [keep.tile([P, S], F32, name=f"y{b}", align_bytes=64) for b in range(3)]
 
         nc.gpsimd.memset(w1s_raw[:].rearrange("p e n -> p (e n)").bitcast(I32), 0)
         nc.gpsimd.memset(x_scales[:].bitcast(I32), 0)
         nc.gpsimd.memset(w2s[:].rearrange("p e n -> p (e n)").bitcast(I32), 0)
+        make_identity(nc, ident[:])
 
         def load_x(c):
             nc.sync.dma_start(out=x_raw[c][:], in_=xT[:, X0[c] : X0[c] + XW[c]].rearrange("(p j) w -> p j w", j=PACK))
@@ -116,8 +117,9 @@ def tile_moe_rag_mlp_relu_kernel(
 
         w1_permute(0)
         w1_permute(1)
+        x_codes = keep.tile([P, T], U32, name="shared", align_bytes=64)
         x_grp = [
-            keep.tile([P, w, PACK], BF16, name="shared" if c == 1 else f"x_grp{c}", align_bytes=64)
+            keep.tile([P, w, PACK], BF16, name=f"x_grp{c}", align_bytes=64)
             for c, w in enumerate(XW)
         ]
         interleave("S", 0, 0, 128)
@@ -131,7 +133,7 @@ def tile_moe_rag_mlp_relu_kernel(
         chunks = [(e, s) for e in range(E) for s in range(0, COUNTS[e], CH)]
         groups = [(0, 4), (4, 8), (8, 10), (10, 12)]
         vector_chunks = (11,)
-        pieces = [(0, 1), (1, 2), (2, 4), (4, 6), (6, 9), (9, 12)]
+        pieces = [(0, 1), (1, 3), (3, 6), (6, 9), (9, 12)]
 
         def bank(k):
             return psum.tile([P, PACK, CH], F32, name=f"bank{k}", bufs=1)
@@ -214,27 +216,45 @@ def tile_moe_rag_mlp_relu_kernel(
                 layer2(b, 4 + k, 4 * k, 4 * k + 4, "S")
 
         def mul(b, r, lo, hi):
-            g = ring.tile([P, T], F32, name=f"m{r}", bufs=4, align_bytes=64)
+            g = keep.tile([P, hi - lo], F32, name=f"m{b}_{r}_{lo}", align_bytes=64)
             pos = (pos1_t, pos2_t)[r]
-            nc.vector.tensor_tensor(
-                g[:, lo:hi], ys[b][:].indirect(pos[:, lo // 16 : hi // 16]), gates[:, r, lo:hi], MULT
-            )
+            nc.vector.tensor_tensor(g[:], ys[b][:].indirect(pos[:, lo // 16 : hi // 16]), gates[:, r, lo:hi], MULT)
             return g
 
-        def finish(b, m1, m2, lo, hi):
-            o = ring.tile([P, T], F32, name="o", bufs=5, align_bytes=64)
-            nc.vector.tensor_tensor(o[:, lo:hi], m1[:, lo:hi], m2[:, lo:hi], ADD)
-            nc.sync.dma_start(out=out[b * P : (b + 1) * P, lo:hi], in_=o[:, lo:hi])
+        def add_on_vector(b, m1, m2, lo, hi):
+            o = keep.tile([P, hi - lo], F32, name=f"o{b}_{lo}", align_bytes=64)
+            nc.vector.tensor_tensor(o[:], m1, m2, ADD)
+            nc.sync.dma_start(out=out[b * P : (b + 1) * P, lo:hi], in_=o[:])
 
-        parts = [(0, 0, T), (1, 0, T), (2, 0, 384), (2, 384, 576), (2, 576, T)]
+        def add_on_tensor(b, m1, m2, lo, hi, bank_turned, bank_back):
+            n = (hi - lo) // P
+            turned = bank(bank_turned)
+            for c in range(n):
+                for r, m in enumerate((m1, m2)):
+                    nc.tensor.matmul(
+                        turned[:, c, :], m[:, c * P : (c + 1) * P], ident[:], start=r == 0, stop=r == 1, is_transpose=True
+                    )
+            z = keep.tile([P, n, P], F32, name=f"z{b}_{lo}", align_bytes=64)
+            nc.scalar.activation(z[:], turned[:, 0:n, :], COPY)
+            back = bank(bank_back)
+            for c in range(n):
+                nc.tensor.transpose(back[:, c, :], z[:, c, :], ident[:])
+            o = keep.tile([P, n, P], F32, name=f"o{b}_{lo}", align_bytes=64)
+            nc.scalar.activation(o[:], back[:, 0:n, :], COPY)
+            nc.scalar.dma_start(out=out[b * P : (b + 1) * P, lo:hi], in_=o[:].rearrange("p c t -> p (c t)"))
+
+        half = T // 2
+        m1, m2 = mul(0, 0, 0, T), mul(0, 1, 0, T)
+        add_on_tensor(0, m1[:, 0:half], m2[:, 0:half], 0, half, 4, 0)
+        add_on_tensor(0, m1[:, half:T], m2[:, half:T], half, T, 5, 1)
+        m1, m2 = mul(1, 0, 0, T), mul(1, 1, 0, T)
+        pending = (1, m1[:], m2[:], 0, T)
+        m1 = mul(2, 0, 0, T)
+        add_on_vector(*pending)
         pending = None
-        for b, lo, hi in parts:
-            m1 = mul(b, 0, lo, hi)
-            if pending is not None and hi < T or b < 2 and pending is not None:
-                finish(*pending)
-                pending = None
-            m2 = mul(b, 1, lo, hi)
+        for lo, hi in ((0, 384), (384, 640), (640, T)):
+            m2 = mul(2, 1, lo, hi)
             if pending is not None:
-                finish(*pending)
-            pending = (b, m1, m2, lo, hi)
-        finish(*pending)
+                add_on_vector(*pending)
+            pending = (2, m1[:, lo:hi], m2[:], lo, hi)
+        add_on_vector(*pending)

@@ -10,8 +10,11 @@ S = 1536
 P = 128
 PACK = 4
 CH = 128
-XW = (128, 256, 256, 128)
-X0 = (0, 128, 384, 640)
+XW = (384, 256, 128)
+X0 = (0, 384, 640)
+X_VECTOR = (192, 160, 80)
+FIRST = 2
+EARLY = 1
 FLOPS = 2 * S * (K * H + H * N)
 
 F32 = mybir.dt.float32
@@ -28,10 +31,20 @@ MULT = mybir.AluOpType.mult
 ADD = mybir.AluOpType.add
 
 
+def widths(n):
+    runs, lo = [], 0
+    for w in (512, 256, 128):
+        while n - lo >= w:
+            runs.append((lo, lo + w))
+            lo = lo + w
+    return runs
+
+
 def tile_moe_rag_mlp_relu_kernel(
     tc, xT, w1_words, w1_scales, w2_words, w2_scales, gate, offs, pos1, pos2, out
 ):
     nc = tc.nc
+    order = [(FIRST + i) % E for i in range(E)]
     with ExitStack() as ctx:
         lists = ctx.enter_context(tc.tile_pool(name="lists", bufs=1))
         keep = ctx.enter_context(tc.tile_pool(name="keep", bufs=1))
@@ -41,8 +54,7 @@ def tile_moe_rag_mlp_relu_kernel(
         pos1_t = lists.tile([P, T // 16], U16, name="pos1_t")
         pos2_t = lists.tile([P, T // 16], U16, name="pos2_t")
 
-        w1_raw = keep.tile([P, E, 2 * H], U8, name="w1_raw", align_bytes=64)
-        w1_codes = keep.tile([P, E, 2 * H], U8, name="w1_codes", align_bytes=64)
+        w1_raw = [keep.tile([P, 2 * H], U8, name=f"w1_raw{e}", align_bytes=64) for e in range(E)]
         w1s_raw = keep.tile([P, E, H], U8, name="shared", align_bytes=64)
         w1s = keep.tile([P, E, H], U8, name="w1s", align_bytes=64)
         w2_codes = keep.tile([P, E, 2 * N], U8, name="w2_codes", align_bytes=64)
@@ -53,32 +65,29 @@ def tile_moe_rag_mlp_relu_kernel(
         ident = keep.tile([P, P], F32, name="ident", align_bytes=64)
         ys = [keep.tile([P, S], F32, name=f"y{b}", align_bytes=64) for b in range(3)]
 
-        nc.gpsimd.memset(w1s_raw[:].rearrange("p e n -> p (e n)").bitcast(I32), 0)
-        nc.gpsimd.memset(x_scales[:].bitcast(I32), 0)
-        nc.gpsimd.memset(w2s[:].rearrange("p e n -> p (e n)").bitcast(I32), 0)
-        make_identity(nc, ident[:])
+        nc.vector.memset(w1s_raw[:].rearrange("p e n -> p (e n)").bitcast(I32), 0)
+        nc.vector.memset(ident[:], 0.0)
+        make_identity(nc, ident[:], nomemset=True)
+        nc.vector.memset(x_scales[:].bitcast(I32), 0)
+        nc.vector.memset(w2s[:].rearrange("p e n -> p (e n)").bitcast(I32), 0)
 
-        def load_x(c):
-            nc.sync.dma_start(out=x_raw[c][:], in_=xT[:, X0[c] : X0[c] + XW[c]].rearrange("(p j) w -> p j w", j=PACK))
-
-        def load_w1(i):
-            nc.sync.dma_start(
-                out=w1_raw[:, 2 * i : 2 * i + 2, :].bitcast(I32),
-                in_=w1_words[2 * i : 2 * i + 2, 0].rearrange("e p b -> p e b").bitcast(I32),
-            )
+        def load_w1(e):
+            nc.sync.dma_start(out=w1_raw[e][:].bitcast(I32), in_=w1_words[e, 0].bitcast(I32))
 
         for q in range(4):
             nc.sync.dma_start(
                 out=w1s_raw[32 * q : 32 * q + 4].bitcast(I32),
                 in_=w1_scales[:, 0, 4 * q : 4 * q + 4, :].rearrange("e q n -> q e n").bitcast(I32),
             )
-        load_w1(0)
-        load_w1(1)
-        load_x(0)
-        load_x(1)
-        load_x(2)
-        load_x(3)
-        nc.sync.dma_start(offs_t[:], offs)
+        for e in order[:EARLY]:
+            load_w1(e)
+
+        for c, w in enumerate(XW):
+            nc.sync.dma_start(out=x_raw[c][:], in_=xT[:, X0[c] : X0[c] + w].rearrange("(p j) w -> p j w", j=PACK))
+            if c == 0:
+                nc.sync.dma_start(offs_t[:], offs)
+        for e in order[EARLY:]:
+            load_w1(e)
         nc.sync.dma_start(out=w2_codes[:].bitcast(I32), in_=w2_words[:, 0].rearrange("e p b -> p e b").bitcast(I32))
         for q in range(4):
             nc.sync.dma_start(
@@ -89,51 +98,52 @@ def tile_moe_rag_mlp_relu_kernel(
         nc.sync.dma_start(pos2_t[:], pos2)
         nc.sync.dma_start(out=gates[:], in_=gate[:, 0:P, :].rearrange("g p t -> p g t"))
 
-        def x_quant(c):
-            nc.vector.quantize_mx(
-                out=x_codes[:, X0[c] : X0[c] + XW[c]].bitcast(FP8X4),
-                scales=x_scales[:, X0[c] : X0[c] + XW[c]],
-                in_=x_grp[c][:].rearrange("p w j -> p (w j)"),
+        w1_codes = {}
+        for e in order[:EARLY]:
+            w1_codes[e] = keep.tile([P, 2 * H], U8, name=f"w1_codes{e}", align_bytes=64)
+            nc.vector.tensor_copy(
+                out=w1_codes[e][:].bitcast(U16).rearrange("p (t m) -> p t m", t=PACK),
+                in_=w1_raw[e][:].bitcast(U16).rearrange("p (m t) -> p t m", t=PACK),
             )
+        nc.vector.tensor_copy(
+            out=w1s[:].rearrange("p e (t m) -> p e t m", t=PACK),
+            in_=w1s_raw[:].rearrange("p e (m t) -> p e t m", t=PACK),
+        )
+        x_codes = keep.tile([P, T], U32, name="shared", align_bytes=64)
+        x_grp = [keep.tile([P, w, PACK], BF16, name=f"x_grp{c}", align_bytes=64) for c, w in enumerate(XW)]
 
-        def interleave(engine, c, lo, hi):
+        def x_quant(c):
+            for lo, hi in widths(XW[c]):
+                nc.vector.quantize_mx(
+                    out=x_codes[:, X0[c] + lo : X0[c] + hi].bitcast(FP8X4),
+                    scales=x_scales[:, X0[c] + lo : X0[c] + hi],
+                    in_=x_grp[c][:, lo:hi, :].rearrange("p w j -> p (w j)"),
+                )
+
+        def interleave(c, lo, hi):
             o = x_grp[c][:, lo:hi, :].rearrange("p (c i) t -> p c t i", i=4)
             i = x_raw[c][:, :, lo:hi].rearrange("p t (c i) -> p c t i", i=4)
-            if engine == "S":
-                nc.scalar.activation(o, i, COPY)
-            else:
-                nc.vector.tensor_copy(o, i)
+            return o, i
 
-        def w1_permute(i):
-            es = slice(2 * i, 2 * i + 2)
-            nc.vector.tensor_copy(
-                out=w1_codes[:, es, :].bitcast(U16).rearrange("p e (t m) -> p e t m", t=PACK),
-                in_=w1_raw[:, es, :].bitcast(U16).rearrange("p e (m t) -> p e t m", t=PACK),
+        for c, w in enumerate(XW):
+            nc.vector.tensor_copy(*interleave(c, 0, X_VECTOR[c]))
+            nc.scalar.activation(*interleave(c, X_VECTOR[c], w), COPY)
+            if c > 0:
+                x_quant(c - 1)
+        x_quant(len(XW) - 1)
+
+        for i, e in enumerate(order[EARLY:]):
+            tag = f"x_grp{len(XW) - 1}" if i == 0 else f"w1_codes{e}"
+            w1_codes[e] = keep.tile([P, 2 * H], U8, name=tag, align_bytes=64)
+            nc.gpsimd.tensor_copy(
+                out=w1_codes[e][:].rearrange("p (t m b) -> p t m b", t=PACK, b=2),
+                in_=w1_raw[e][:].rearrange("p (m t b) -> p t m b", t=PACK, b=2),
             )
-            nc.vector.tensor_copy(
-                out=w1s[:, es, :].rearrange("p e (t m) -> p e t m", t=PACK),
-                in_=w1s_raw[:, es, :].rearrange("p e (m t) -> p e t m", t=PACK),
-            )
 
-        w1_permute(0)
-        w1_permute(1)
-        x_codes = keep.tile([P, T], U32, name="shared", align_bytes=64)
-        x_grp = [
-            keep.tile([P, w, PACK], BF16, name=f"x_grp{c}", align_bytes=64)
-            for c, w in enumerate(XW)
-        ]
-        interleave("S", 0, 0, 128)
-        for c in (1, 2, 3):
-            cut = XW[c] * 5 // 8
-            interleave("V", c, 0, cut)
-            interleave("S", c, cut, XW[c])
-            x_quant(c - 1)
-        x_quant(3)
-
-        chunks = [(e, s) for e in range(E) for s in range(0, COUNTS[e], CH)]
-        groups = [(0, 4), (4, 8), (8, 10), (10, 12)]
+        chunks = [(e, STARTS[e] + s) for e in order for s in range(0, COUNTS[e], CH)]
+        groups = ((0, 4), (4, 8), (8, 10), (10, 12))
         vector_chunks = (11,)
-        pieces = [(0, 1), (1, 3), (3, 6), (6, 9), (9, 12)]
+        pieces = ((0, 1), (1, 2), (2, 4), (4, 7), (7, 10), (10, 12))
 
         def bank(k):
             return psum.tile([P, PACK, CH], F32, name=f"bank{k}", bufs=1)
@@ -142,7 +152,7 @@ def tile_moe_rag_mlp_relu_kernel(
         for lo, hi in pieces:
             words = keep.tile([P, (hi - lo) * CH], U32, name=f"xg{lo}", align_bytes=64)
             bytes_ = keep.tile([P, (hi - lo) * CH], U8, name=f"xgs{lo}", align_bytes=64)
-            cols = slice(lo * CH // 16, hi * CH // 16)
+            cols = slice(chunks[lo][1] // 16, chunks[lo][1] // 16 + (hi - lo) * CH // 16)
             nc.vector.tensor_copy(words[:], x_codes[:].indirect(offs_t[:, cols]))
             nc.vector.tensor_copy(bytes_[:], x_scales[:].indirect(offs_t[:, cols]))
             for c in range(lo, hi):
@@ -158,7 +168,7 @@ def tile_moe_rag_mlp_relu_kernel(
                 for t in range(PACK):
                     nc.tensor.matmul_mx(
                         out=acc[:, t, :],
-                        lhsT=w1_codes[:, e, 256 * t : 256 * t + 256].bitcast(FP4X4),
+                        lhsT=w1_codes[e][:, 256 * t : 256 * t + 256].bitcast(FP4X4),
                         lhsT_scale=w1s[:, e, 128 * t : 128 * t + 128],
                         rhs=xg[c].bitcast(FP8X4),
                         rhs_scale=xgs[c],
@@ -182,18 +192,21 @@ def tile_moe_rag_mlp_relu_kernel(
                 in_=h_grp[lo][:].rearrange("p n t -> p (n t)"),
             )
 
-        runs = [(0, 2), (2, 4), (4, 5), (5, 7), (7, 8), (8, 9), (9, 10), (10, 12)]
-
-        def layer2(b, k, first, last, engine):
-            yp = bank(k)
-            flat = yp[:].rearrange("p t n -> p (t n)")
-            for lo, hi in runs:
-                if first <= lo < last:
-                    e = chunks[lo][0]
-                    g = max(g for g, g_end in groups if g <= lo)
-                    cols = slice((lo - g) * CH, (hi - g) * CH)
+        def layer2(b, k, members, engine):
+            flat = bank(k)[:].rearrange("p t n -> p (t n)")
+            runs = []
+            for c in members:
+                g = max(g for g, g_end in groups if g <= c)
+                if runs and runs[-1][0] == (g, chunks[c][0]) and runs[-1][1][-1] == c - 1:
+                    runs[-1][1].append(c)
+                else:
+                    runs.append(((g, chunks[c][0]), [c]))
+            at = 0
+            for (g, e), cs in runs:
+                for lo, hi in widths(len(cs) * CH):
+                    cols = slice((cs[0] - g) * CH + lo, (cs[0] - g) * CH + hi)
                     nc.tensor.matmul_mx(
-                        out=flat[:, (lo - first) * CH : (hi - first) * CH],
+                        out=flat[:, at + lo : at + hi],
                         lhsT=w2_codes[:, e, 256 * b : 256 * b + 256].bitcast(FP4X4),
                         lhsT_scale=w2s[:, e, 128 * b : 128 * b + 128],
                         rhs=h_codes[g][:, cols].bitcast(FP8X4),
@@ -201,19 +214,20 @@ def tile_moe_rag_mlp_relu_kernel(
                         start=True,
                         stop=True,
                     )
-            o, i = ys[b][:, first * CH : last * CH], flat[:, 0 : (last - first) * CH]
+                at = at + len(cs) * CH
+            first = chunks[members[0]][1]
+            o, i = ys[b][:, first : first + at], flat[:, 0:at]
             if engine == "S":
                 nc.scalar.activation(o, i, COPY)
             else:
                 nc.vector.tensor_copy(o, i)
 
-        layer2(0, 4, 0, 4, "S")
-        layer2(0, 5, 4, 8, "S")
-        layer2(0, 2, 8, 10, "V")
-        layer2(0, 7, 10, 12, "V")
+        for lo, hi, k, engine in ((0, 4, 4, "S"), (4, 7, 5, "S"), (7, 8, 6, "S"), (8, 10, 2, "V"), (10, 12, 7, "V")):
+            layer2(0, k, list(range(lo, hi)), engine)
+        by_slot = sorted(range(len(chunks)), key=lambda c: chunks[c][1])
         for b in (1, 2):
             for k in range(3):
-                layer2(b, 4 + k, 4 * k, 4 * k + 4, "S")
+                layer2(b, 4 + k, by_slot[4 * k : 4 * k + 4], "S")
 
         def mul(b, r, lo, hi):
             g = keep.tile([P, hi - lo], F32, name=f"m{b}_{r}_{lo}", align_bytes=64)

@@ -136,8 +136,8 @@ def tile_moe_rag_mlp_relu_kernel(
             tag = f"x_grp{len(XW) - 1}" if i == 0 else f"w1_codes{e}"
             w1_codes[e] = keep.tile([P, 2 * H], U8, name=tag, align_bytes=64)
             nc.gpsimd.tensor_copy(
-                out=w1_codes[e][:].rearrange("p (t m b) -> p t m b", t=PACK, b=2),
-                in_=w1_raw[e][:].rearrange("p (m t b) -> p t m b", t=PACK, b=2),
+                out=w1_codes[e][:].bitcast(U16).rearrange("p (t m) -> p t m", t=PACK),
+                in_=w1_raw[e][:].bitcast(U16).rearrange("p (m t) -> p t m", t=PACK),
             )
 
         chunks = [(e, STARTS[e] + s) for e in order for s in range(0, COUNTS[e], CH)]

@@ -12,8 +12,8 @@ PACK = 4
 CH = 128
 XW = (384, 256, 128)
 X0 = (0, 384, 640)
-X_VECTOR = (192, 160, 80)
-FIRST = 2
+X_VECTOR = (208, 160, 80)
+FIRST = 3
 EARLY = 1
 FLOPS = 2 * S * (K * H + H * N)
 
@@ -48,15 +48,18 @@ def tile_moe_rag_mlp_relu_kernel(
     with ExitStack() as ctx:
         lists = ctx.enter_context(tc.tile_pool(name="lists", bufs=1))
         keep = ctx.enter_context(tc.tile_pool(name="keep", bufs=1))
+        early = ctx.enter_context(tc.tile_pool(name="early", bufs=1))
         psum = ctx.enter_context(tc.psum_pool(name="psum", bufs=1))
 
         offs_t = lists.tile([P, 2 * T // 16], U16, name="offs_t")
         pos1_t = lists.tile([P, T // 16], U16, name="pos1_t")
         pos2_t = lists.tile([P, T // 16], U16, name="pos2_t")
 
-        w1_raw = [keep.tile([P, 2 * H], U8, name=f"w1_raw{e}", align_bytes=64) for e in range(E)]
-        w1s_raw = keep.tile([P, E, H], U8, name="shared", align_bytes=64)
-        w1s = keep.tile([P, E, H], U8, name="w1s", align_bytes=64)
+        w1_raw = {e: keep.tile([P, 2 * H], U8, name=f"w1_raw{e}", align_bytes=64)[:] for e in order[1:]}
+        held = S - CH
+        first_raw = early.tile([P, 3 * H], U8, name="first_raw", offset=4 * held - H, align_bytes=64)
+        w1s_first, w1_raw[FIRST] = first_raw[:, 0:H], first_raw[:, H : 3 * H]
+        w1s_raw = keep.tile([P, E - 1, H], U8, name="w1s_raw", align_bytes=64)
         w2_codes = keep.tile([P, E, 2 * N], U8, name="w2_codes", align_bytes=64)
         w2s = keep.tile([P, E, N], U8, name="w2s", align_bytes=64)
         x_raw = [keep.tile([P, PACK, w], F32, name=f"x_raw{c}", align_bytes=64) for c, w in enumerate(XW)]
@@ -65,6 +68,7 @@ def tile_moe_rag_mlp_relu_kernel(
         ident = keep.tile([P, P], F32, name="ident", align_bytes=64)
         ys = [keep.tile([P, S], F32, name=f"y{b}", align_bytes=64) for b in range(3)]
 
+        nc.vector.memset(w1s_first.bitcast(I32), 0)
         nc.vector.memset(w1s_raw[:].rearrange("p e n -> p (e n)").bitcast(I32), 0)
         nc.vector.memset(ident[:], 0.0)
         make_identity(nc, ident[:], nomemset=True)
@@ -72,22 +76,24 @@ def tile_moe_rag_mlp_relu_kernel(
         nc.vector.memset(w2s[:].rearrange("p e n -> p (e n)").bitcast(I32), 0)
 
         def load_w1(e):
-            nc.sync.dma_start(out=w1_raw[e][:].bitcast(I32), in_=w1_words[e, 0].bitcast(I32))
-
-        for q in range(4):
-            nc.sync.dma_start(
-                out=w1s_raw[32 * q : 32 * q + 4].bitcast(I32),
-                in_=w1_scales[:, 0, 4 * q : 4 * q + 4, :].rearrange("e q n -> q e n").bitcast(I32),
-            )
-        for e in order[:EARLY]:
-            load_w1(e)
+            nc.sync.dma_start(out=w1_raw[e].bitcast(I32), in_=w1_words[e, 0].bitcast(I32))
 
         for c, w in enumerate(XW):
             nc.sync.dma_start(out=x_raw[c][:], in_=xT[:, X0[c] : X0[c] + w].rearrange("(p j) w -> p j w", j=PACK))
-            if c == 0:
-                nc.sync.dma_start(offs_t[:], offs)
-        for e in order[EARLY:]:
-            load_w1(e)
+        nc.sync.dma_start(offs_t[:], offs)
+        for q in range(4):
+            nc.sync.dma_start(
+                out=w1s_first[32 * q : 32 * q + 4].bitcast(I32), in_=w1_scales[FIRST, 0, 4 * q : 4 * q + 4, :].bitcast(I32)
+            )
+        load_w1(order[0])
+        load_w1(order[1])
+        for q in range(4):
+            nc.sync.dma_start(
+                out=w1s_raw[32 * q : 32 * q + 4].bitcast(I32),
+                in_=w1_scales[0 : E - 1, 0, 4 * q : 4 * q + 4, :].rearrange("e q n -> q e n").bitcast(I32),
+            )
+        load_w1(order[2])
+        load_w1(order[3])
         nc.sync.dma_start(out=w2_codes[:].bitcast(I32), in_=w2_words[:, 0].rearrange("e p b -> p e b").bitcast(I32))
         for q in range(4):
             nc.sync.dma_start(
@@ -98,18 +104,7 @@ def tile_moe_rag_mlp_relu_kernel(
         nc.sync.dma_start(pos2_t[:], pos2)
         nc.sync.dma_start(out=gates[:], in_=gate[:, 0:P, :].rearrange("g p t -> p g t"))
 
-        w1_codes = {}
-        for e in order[:EARLY]:
-            w1_codes[e] = keep.tile([P, 2 * H], U8, name=f"w1_codes{e}", align_bytes=64)
-            nc.vector.tensor_copy(
-                out=w1_codes[e][:].bitcast(U16).rearrange("p (t m) -> p t m", t=PACK),
-                in_=w1_raw[e][:].bitcast(U16).rearrange("p (m t) -> p t m", t=PACK),
-            )
-        nc.vector.tensor_copy(
-            out=w1s[:].rearrange("p e (t m) -> p e t m", t=PACK),
-            in_=w1s_raw[:].rearrange("p e (m t) -> p e t m", t=PACK),
-        )
-        x_codes = keep.tile([P, T], U32, name="shared", align_bytes=64)
+        x_codes = keep.tile([P, T], U32, name="x_codes", align_bytes=64)
         x_grp = [keep.tile([P, w, PACK], BF16, name=f"x_grp{c}", align_bytes=64) for c, w in enumerate(XW)]
 
         def x_quant(c):
@@ -132,29 +127,43 @@ def tile_moe_rag_mlp_relu_kernel(
                 x_quant(c - 1)
         x_quant(len(XW) - 1)
 
-        for i, e in enumerate(order[EARLY:]):
-            tag = f"x_grp{len(XW) - 1}" if i == 0 else f"w1_codes{e}"
-            w1_codes[e] = keep.tile([P, 2 * H], U8, name=tag, align_bytes=64)
-            nc.gpsimd.tensor_copy(
-                out=w1_codes[e][:].bitcast(U16).rearrange("p (t m) -> p t m", t=PACK),
-                in_=w1_raw[e][:].bitcast(U16).rearrange("p (m t) -> p t m", t=PACK),
+        w1_codes, w1s = {}, {}
+        late = keep.tile([P, (E - 1) * 3 * H], U8, name=f"x_grp{len(XW) - 1}", align_bytes=64)
+        for i, e in enumerate(order):
+            if i == 0:
+                engine, raw_scales = nc.vector, w1s_first
+                both = keep.tile([P, 3 * H], U8, name="w1_first", align_bytes=64)[:]
+            else:
+                engine, raw_scales = nc.gpsimd, w1s_raw[:, e, :]
+                both = late[:, (i - 1) * 3 * H : i * 3 * H]
+            w1_codes[e], w1s[e] = both[:, 0 : 2 * H], both[:, 2 * H : 3 * H]
+            engine.tensor_copy(w1s[e].rearrange("p (t m) -> p t m", t=PACK), raw_scales.rearrange("p (m t) -> p t m", t=PACK))
+            engine.tensor_copy(
+                w1_codes[e].bitcast(U16).rearrange("p (t m) -> p t m", t=PACK),
+                w1_raw[e].bitcast(U16).rearrange("p (m t) -> p t m", t=PACK),
             )
 
         chunks = [(e, STARTS[e] + s) for e in order for s in range(0, COUNTS[e], CH)]
         groups = ((0, 4), (4, 8), (8, 10), (10, 12))
         vector_chunks = (11,)
-        pieces = ((0, 1), (1, 2), (2, 4), (4, 7), (7, 10), (10, 12))
+        pieces = ((0, 1), (1, 3), (3, 5), (5, 8), (8, 10), (10, 12))
 
         def bank(k):
             return psum.tile([P, PACK, CH], F32, name=f"bank{k}", bufs=1)
 
         xg, xgs = {}, {}
+        first_words = keep.tile([P, CH], U32, name="first_words", align_bytes=64)
+        first_bytes = keep.tile([P, CH], U8, name="first_bytes", align_bytes=64)
+        held_words = early.tile([P, held], U32, name="held_words", offset=0, align_bytes=64)
+        held_bytes = early.tile([P, held], U8, name="held_bytes", offset=4 * held, align_bytes=64)
         for lo, hi in pieces:
-            words = keep.tile([P, (hi - lo) * CH], U32, name=f"xg{lo}", align_bytes=64)
-            bytes_ = keep.tile([P, (hi - lo) * CH], U8, name=f"xgs{lo}", align_bytes=64)
+            if lo == 0:
+                words, bytes_ = first_words[:], first_bytes[:]
+            else:
+                words, bytes_ = held_words[:, (lo - 1) * CH : (hi - 1) * CH], held_bytes[:, (lo - 1) * CH : (hi - 1) * CH]
             cols = slice(chunks[lo][1] // 16, chunks[lo][1] // 16 + (hi - lo) * CH // 16)
-            nc.vector.tensor_copy(words[:], x_codes[:].indirect(offs_t[:, cols]))
-            nc.vector.tensor_copy(bytes_[:], x_scales[:].indirect(offs_t[:, cols]))
+            nc.vector.tensor_copy(words, x_codes[:].indirect(offs_t[:, cols]))
+            nc.vector.tensor_copy(bytes_, x_scales[:].indirect(offs_t[:, cols]))
             for c in range(lo, hi):
                 xg[c] = words[:, (c - lo) * CH : (c - lo + 1) * CH]
                 xgs[c] = bytes_[:, (c - lo) * CH : (c - lo + 1) * CH]
@@ -169,7 +178,7 @@ def tile_moe_rag_mlp_relu_kernel(
                     nc.tensor.matmul_mx(
                         out=acc[:, t, :],
                         lhsT=w1_codes[e][:, 256 * t : 256 * t + 256].bitcast(FP4X4),
-                        lhsT_scale=w1s[:, e, 128 * t : 128 * t + 128],
+                        lhsT_scale=w1s[e][:, 128 * t : 128 * t + 128],
                         rhs=xg[c].bitcast(FP8X4),
                         rhs_scale=xgs[c],
                         start=True,
@@ -222,7 +231,7 @@ def tile_moe_rag_mlp_relu_kernel(
             else:
                 nc.vector.tensor_copy(o, i)
 
-        for lo, hi, k, engine in ((0, 4, 4, "S"), (4, 7, 5, "S"), (7, 8, 6, "S"), (8, 10, 2, "V"), (10, 12, 7, "V")):
+        for lo, hi, k, engine in ((0, 3, 4, "S"), (3, 7, 5, "S"), (7, 8, 6, "S"), (8, 10, 2, "V"), (10, 12, 7, "V")):
             layer2(0, k, list(range(lo, hi)), engine)
         by_slot = sorted(range(len(chunks)), key=lambda c: chunks[c][1])
         for b in (1, 2):

@@ -270,10 +270,10 @@ def tile_moe_rag_mlp_relu_kernel(
         m1, m2 = mul(0, 0, 0, T), mul(0, 1, 0, T)
         add_on_tensor(0, m1[:, 0:half], m2[:, 0:half], 0, half, 4, 0)
         add_on_tensor(0, m1[:, half:T], m2[:, half:T], half, T, 5, 1)
-        m1, m2 = mul(1, 0, 0, T), mul(1, 1, 0, T)
-        pending = (1, m1[:], m2[:], 0, T)
+        for k, (lo, hi) in enumerate(((0, half), (half, T))):
+            m1, m2 = mul(1, 0, lo, hi), mul(1, 1, lo, hi)
+            add_on_tensor(1, m1[:], m2[:], lo, hi, 4 + k, k)
         m1 = mul(2, 0, 0, T)
-        add_on_vector(*pending)
         pending = None
         for lo, hi in ((0, 384), (384, 640), (640, T)):
             m2 = mul(2, 1, lo, hi)

@@ -14,7 +14,6 @@ XW = (384, 256, 128)
 X0 = (0, 384, 640)
 X_VECTOR = (208, 160, 80)
 FIRST = 3
-EARLY = 1
 FLOPS = 2 * S * (K * H + H * N)
 
 F32 = mybir.dt.float32
@@ -44,7 +43,7 @@ def tile_moe_rag_mlp_relu_kernel(
     tc, xT, w1_words, w1_scales, w2_words, w2_scales, gate, offs, pos1, pos2, out
 ):
     nc = tc.nc
-    order = [(FIRST + i) % E for i in range(E)]
+    order = [FIRST - i for i in range(E)]
     with ExitStack() as ctx:
         lists = ctx.enter_context(tc.tile_pool(name="lists", bufs=1))
         keep = ctx.enter_context(tc.tile_pool(name="keep", bufs=1))
@@ -57,7 +56,7 @@ def tile_moe_rag_mlp_relu_kernel(
 
         w1_raw = {e: keep.tile([P, 2 * H], U8, name=f"w1_raw{e}", align_bytes=64)[:] for e in order[1:]}
         held = S - CH
-        first_raw = early.tile([P, 3 * H], U8, name="first_raw", offset=4 * held - H, align_bytes=64)
+        first_raw = early.tile([P, 3 * H], U8, name="first_raw", offset=4 * held - 64, align_bytes=64)
         w1s_first, w1_raw[FIRST] = first_raw[:, 0:H], first_raw[:, H : 3 * H]
         w1s_raw = keep.tile([P, E - 1, H], U8, name="w1s_raw", align_bytes=64)
         w2_codes = keep.tile([P, E, 2 * N], U8, name="w2_codes", align_bytes=64)
@@ -80,12 +79,12 @@ def tile_moe_rag_mlp_relu_kernel(
 
         for c, w in enumerate(XW):
             nc.sync.dma_start(out=x_raw[c][:], in_=xT[:, X0[c] : X0[c] + w].rearrange("(p j) w -> p j w", j=PACK))
+        load_w1(order[0])
         nc.sync.dma_start(offs_t[:], offs)
         for q in range(4):
             nc.sync.dma_start(
                 out=w1s_first[32 * q : 32 * q + 4].bitcast(I32), in_=w1_scales[FIRST, 0, 4 * q : 4 * q + 4, :].bitcast(I32)
             )
-        load_w1(order[0])
         load_w1(order[1])
         for q in range(4):
             nc.sync.dma_start(
@@ -128,7 +127,7 @@ def tile_moe_rag_mlp_relu_kernel(
         x_quant(len(XW) - 1)
 
         w1_codes, w1s = {}, {}
-        late = keep.tile([P, (E - 1) * 3 * H], U8, name=f"x_grp{len(XW) - 1}", align_bytes=64)
+        late = early.tile([P, (E - 1) * 3 * H], U8, name="late", offset=5 * held, align_bytes=64)
         for i, e in enumerate(order):
             if i == 0:
                 engine, raw_scales = nc.vector, w1s_first
@@ -137,50 +136,50 @@ def tile_moe_rag_mlp_relu_kernel(
                 engine, raw_scales = nc.gpsimd, w1s_raw[:, e, :]
                 both = late[:, (i - 1) * 3 * H : i * 3 * H]
             w1_codes[e], w1s[e] = both[:, 0 : 2 * H], both[:, 2 * H : 3 * H]
-            engine.tensor_copy(w1s[e].rearrange("p (t m) -> p t m", t=PACK), raw_scales.rearrange("p (m t) -> p t m", t=PACK))
             engine.tensor_copy(
                 w1_codes[e].bitcast(U16).rearrange("p (t m) -> p t m", t=PACK),
                 w1_raw[e].bitcast(U16).rearrange("p (m t) -> p t m", t=PACK),
             )
+            engine.tensor_copy(w1s[e].rearrange("p (t m) -> p t m", t=PACK), raw_scales.rearrange("p (m t) -> p t m", t=PACK))
 
-        chunks = [(e, STARTS[e] + s) for e in order for s in range(0, COUNTS[e], CH)]
-        groups = ((0, 4), (4, 8), (8, 10), (10, 12))
-        vector_chunks = (11,)
-        pieces = ((0, 1), (1, 3), (3, 5), (5, 8), (8, 10), (10, 12))
+        expert = [e for e in range(E) for s in range(0, COUNTS[e], CH)]
+        groups = ((8, 12), (4, 8), (2, 4), (0, 2))
+        vector_chunks = (2,)
+        pieces = ((11, 12), (9, 11), (7, 9), (4, 7), (2, 4), (0, 2))
 
         def bank(k):
             return psum.tile([P, PACK, CH], F32, name=f"bank{k}", bufs=1)
 
-        xg, xgs = {}, {}
         first_words = keep.tile([P, CH], U32, name="first_words", align_bytes=64)
         first_bytes = keep.tile([P, CH], U8, name="first_bytes", align_bytes=64)
         held_words = early.tile([P, held], U32, name="held_words", offset=0, align_bytes=64)
         held_bytes = early.tile([P, held], U8, name="held_bytes", offset=4 * held, align_bytes=64)
+
+        def gathered(lo, hi):
+            if lo * CH == held:
+                return first_words[:], first_bytes[:]
+            return held_words[:, lo * CH : hi * CH], held_bytes[:, lo * CH : hi * CH]
+
         for lo, hi in pieces:
-            if lo == 0:
-                words, bytes_ = first_words[:], first_bytes[:]
-            else:
-                words, bytes_ = held_words[:, (lo - 1) * CH : (hi - 1) * CH], held_bytes[:, (lo - 1) * CH : (hi - 1) * CH]
-            cols = slice(chunks[lo][1] // 16, chunks[lo][1] // 16 + (hi - lo) * CH // 16)
+            words, bytes_ = gathered(lo, hi)
+            cols = slice(lo * CH // 16, hi * CH // 16)
             nc.vector.tensor_copy(words, x_codes[:].indirect(offs_t[:, cols]))
             nc.vector.tensor_copy(bytes_, x_scales[:].indirect(offs_t[:, cols]))
-            for c in range(lo, hi):
-                xg[c] = words[:, (c - lo) * CH : (c - lo + 1) * CH]
-                xgs[c] = bytes_[:, (c - lo) * CH : (c - lo + 1) * CH]
 
         h_grp = {}
         for lo, hi in groups:
             h_grp[lo] = keep.tile([P, (hi - lo) * CH, PACK], BF16, name=f"h_grp{lo}", align_bytes=64)
-            for c in range(lo, hi):
-                e = chunks[c][0]
-                acc = bank(c % 8)
+            for c in reversed(range(lo, hi)):
+                e = expert[c]
+                words, bytes_ = gathered(c, c + 1)
+                acc = bank((len(expert) - 1 - c) % 8)
                 for t in range(PACK):
                     nc.tensor.matmul_mx(
                         out=acc[:, t, :],
                         lhsT=w1_codes[e][:, 256 * t : 256 * t + 256].bitcast(FP4X4),
                         lhsT_scale=w1s[e][:, 128 * t : 128 * t + 128],
-                        rhs=xg[c].bitcast(FP8X4),
-                        rhs_scale=xgs[c],
+                        rhs=words.bitcast(FP8X4),
+                        rhs_scale=bytes_,
                         start=True,
                         stop=True,
                     )
@@ -201,42 +200,33 @@ def tile_moe_rag_mlp_relu_kernel(
                 in_=h_grp[lo][:].rearrange("p n t -> p (n t)"),
             )
 
-        def layer2(b, k, members, engine):
+        def layer2(b, first, last, k, engine):
             flat = bank(k)[:].rearrange("p t n -> p (t n)")
-            runs = []
-            for c in members:
-                g = max(g for g, g_end in groups if g <= c)
-                if runs and runs[-1][0] == (g, chunks[c][0]) and runs[-1][1][-1] == c - 1:
-                    runs[-1][1].append(c)
-                else:
-                    runs.append(((g, chunks[c][0]), [c]))
-            at = 0
-            for (g, e), cs in runs:
-                for lo, hi in widths(len(cs) * CH):
-                    cols = slice((cs[0] - g) * CH + lo, (cs[0] - g) * CH + hi)
-                    nc.tensor.matmul_mx(
-                        out=flat[:, at + lo : at + hi],
-                        lhsT=w2_codes[:, e, 256 * b : 256 * b + 256].bitcast(FP4X4),
-                        lhsT_scale=w2s[:, e, 128 * b : 128 * b + 128],
-                        rhs=h_codes[g][:, cols].bitcast(FP8X4),
-                        rhs_scale=h_scales[g][:, cols],
-                        start=True,
-                        stop=True,
-                    )
-                at = at + len(cs) * CH
-            first = chunks[members[0]][1]
-            o, i = ys[b][:, first : first + at], flat[:, 0:at]
+            for g, g_end in groups:
+                for e in order:
+                    cs = [c for c in range(max(first, g), min(last, g_end)) if expert[c] == e]
+                    for lo, hi in widths(len(cs) * CH):
+                        cols = slice((cs[0] - g) * CH + lo, (cs[0] - g) * CH + hi)
+                        nc.tensor.matmul_mx(
+                            out=flat[:, (cs[0] - first) * CH + lo : (cs[0] - first) * CH + hi],
+                            lhsT=w2_codes[:, e, 256 * b : 256 * b + 256].bitcast(FP4X4),
+                            lhsT_scale=w2s[:, e, 128 * b : 128 * b + 128],
+                            rhs=h_codes[g][:, cols].bitcast(FP8X4),
+                            rhs_scale=h_scales[g][:, cols],
+                            start=True,
+                            stop=True,
+                        )
+            o, i = ys[b][:, first * CH : last * CH], flat[:, 0 : (last - first) * CH]
             if engine == "S":
                 nc.scalar.activation(o, i, COPY)
             else:
                 nc.vector.tensor_copy(o, i)
 
-        for lo, hi, k, engine in ((0, 3, 4, "S"), (3, 7, 5, "S"), (7, 8, 6, "S"), (8, 10, 2, "V"), (10, 12, 7, "V")):
-            layer2(0, k, list(range(lo, hi)), engine)
-        by_slot = sorted(range(len(chunks)), key=lambda c: chunks[c][1])
+        for lo, hi, k, engine in ((8, 12, 0, "S"), (4, 8, 1, "S"), (2, 4, 2, "V"), (0, 2, 7, "V")):
+            layer2(0, lo, hi, k, engine)
         for b in (1, 2):
             for k in range(3):
-                layer2(b, 4 + k, by_slot[4 * k : 4 * k + 4], "S")
+                layer2(b, 8 - 4 * k, 12 - 4 * k, (0, 1, 3)[k], "S")
 
         def mul(b, r, lo, hi):
             g = keep.tile([P, hi - lo], F32, name=f"m{b}_{r}_{lo}", align_bytes=64)
@@ -268,12 +258,12 @@ def tile_moe_rag_mlp_relu_kernel(
 
         half = T // 2
         m1, m2 = mul(0, 0, 0, T), mul(0, 1, 0, T)
-        add_on_tensor(0, m1[:, 0:half], m2[:, 0:half], 0, half, 4, 0)
-        add_on_tensor(0, m1[:, half:T], m2[:, half:T], half, T, 5, 1)
-        for k, (lo, hi) in enumerate(((0, half), (half, T))):
-            m1, m2 = mul(1, 0, lo, hi), mul(1, 1, lo, hi)
-            add_on_tensor(1, m1[:], m2[:], lo, hi, 4 + k, k)
+        add_on_tensor(0, m1[:, 0:half], m2[:, 0:half], 0, half, 0, 4)
+        add_on_tensor(0, m1[:, half:T], m2[:, half:T], half, T, 1, 5)
+        m1, m2 = mul(1, 0, 0, T), mul(1, 1, 0, T)
+        pending = (1, m1[:], m2[:], 0, T)
         m1 = mul(2, 0, 0, T)
+        add_on_vector(*pending)
         pending = None
         for lo, hi in ((0, 384), (384, 640), (640, T)):
             m2 = mul(2, 1, lo, hi)

@@ -144,7 +144,7 @@ def tile_moe_rag_mlp_relu_kernel(
 
         expert = [e for e in range(E) for s in range(0, COUNTS[e], CH)]
         groups = ((8, 12), (4, 8), (2, 4), (0, 2))
-        vector_chunks = (2,)
+        vector_chunks = (4, 2)
         pieces = ((11, 12), (9, 11), (7, 9), (4, 7), (2, 4), (0, 2))
 
         def bank(k):

@@ -145,7 +145,7 @@ def tile_moe_rag_mlp_relu_kernel(
         expert = [e for e in range(E) for s in range(0, COUNTS[e], CH)]
         groups = ((8, 12), (4, 8), (2, 4), (0, 2))
         vector_chunks = (4, 2)
-        pieces = ((11, 12), (9, 11), (7, 9), (4, 7), (2, 4), (0, 2))
+        pieces = ((11, 12), (9, 11), (6, 9), (3, 6), (0, 3))
 
         def bank(k):
             return psum.tile([P, PACK, CH], F32, name=f"bank{k}", bufs=1)
@@ -166,29 +166,37 @@ def tile_moe_rag_mlp_relu_kernel(
             nc.vector.tensor_copy(words, x_codes[:].indirect(offs_t[:, cols]))
             nc.vector.tensor_copy(bytes_, x_scales[:].indirect(offs_t[:, cols]))
 
-        h_grp = {}
-        for lo, hi in groups:
-            h_grp[lo] = keep.tile([P, (hi - lo) * CH, PACK], BF16, name=f"h_grp{lo}", align_bytes=64)
-            for c in reversed(range(lo, hi)):
-                e = expert[c]
-                words, bytes_ = gathered(c, c + 1)
-                acc = bank((len(expert) - 1 - c) % 8)
-                for t in range(PACK):
-                    nc.tensor.matmul_mx(
-                        out=acc[:, t, :],
-                        lhsT=w1_codes[e][:, 256 * t : 256 * t + 256].bitcast(FP4X4),
-                        lhsT_scale=w1s[e][:, 128 * t : 128 * t + 128],
-                        rhs=words.bitcast(FP8X4),
-                        rhs_scale=bytes_,
-                        start=True,
-                        stop=True,
-                    )
-                o = h_grp[lo][:, (c - lo) * CH : (c - lo + 1) * CH, :]
-                a = acc[:].rearrange("p t n -> p n t")
-                if c in vector_chunks:
-                    nc.vector.tensor_scalar_max(o, a, 0.0)
-                else:
-                    nc.scalar.activation(o, a, RELU)
+        h_grp = {lo: keep.tile([P, (hi - lo) * CH, PACK], BF16, name=f"h_grp{lo}", align_bytes=64) for lo, hi in groups}
+
+        def layer1(c):
+            e = expert[c]
+            words, bytes_ = gathered(c, c + 1)
+            acc = bank((len(expert) - 1 - c) % 8)
+            for t in range(PACK):
+                nc.tensor.matmul_mx(
+                    out=acc[:, t, :],
+                    lhsT=w1_codes[e][:, 256 * t : 256 * t + 256].bitcast(FP4X4),
+                    lhsT_scale=w1s[e][:, 128 * t : 128 * t + 128],
+                    rhs=words.bitcast(FP8X4),
+                    rhs_scale=bytes_,
+                    start=True,
+                    stop=True,
+                )
+            return acc
+
+        def relu(c, acc):
+            g = max(g for g, g_end in groups if g <= c)
+            o = h_grp[g][:, (c - g) * CH : (c - g + 1) * CH, :]
+            a = acc[:].rearrange("p t n -> p n t")
+            if c in vector_chunks:
+                nc.vector.tensor_scalar_max(o, a, 0.0)
+            else:
+                nc.scalar.activation(o, a, RELU)
+
+        for run in ((11,), (10,), (9,), (8, 7), (6, 5), (4,), (3,), (2,), (1, 0)):
+            sums = [(c, layer1(c)) for c in run]
+            for c, acc in reversed(sums):
+                relu(c, acc)
 
         h_codes, h_scales = {}, {}
         for lo, hi in groups:
@@ -218,7 +226,7 @@ def tile_moe_rag_mlp_relu_kernel(
                         )
             o, i = ys[b][:, first * CH : last * CH], flat[:, 0 : (last - first) * CH]
             if engine == "S":
-                nc.scalar.activation(o, i, COPY)
+                nc.scalar.copy(o, i)
             else:
                 nc.vector.tensor_copy(o, i)
 
@@ -248,20 +256,21 @@ def tile_moe_rag_mlp_relu_kernel(
                         turned[:, c, :], m[:, c * P : (c + 1) * P], ident[:], start=r == 0, stop=r == 1, is_transpose=True
                     )
             z = keep.tile([P, n, P], F32, name=f"z{b}_{lo}", align_bytes=64)
-            nc.scalar.activation(z[:], turned[:, 0:n, :], COPY)
+            nc.scalar.copy(z[:], turned[:, 0:n, :])
             back = bank(bank_back)
             for c in range(n):
                 nc.tensor.transpose(back[:, c, :], z[:, c, :], ident[:])
             o = keep.tile([P, n, P], F32, name=f"o{b}_{lo}", align_bytes=64)
-            nc.scalar.activation(o[:], back[:, 0:n, :], COPY)
+            nc.scalar.copy(o[:], back[:, 0:n, :])
             nc.scalar.dma_start(out=out[b * P : (b + 1) * P, lo:hi], in_=o[:].rearrange("p c t -> p (c t)"))
 
         half = T // 2
-        m1, m2 = mul(0, 0, 0, T), mul(0, 1, 0, T)
-        add_on_tensor(0, m1[:, 0:half], m2[:, 0:half], 0, half, 0, 4)
-        add_on_tensor(0, m1[:, half:T], m2[:, half:T], half, T, 1, 5)
-        m1, m2 = mul(1, 0, 0, T), mul(1, 1, 0, T)
-        pending = (1, m1[:], m2[:], 0, T)
+        halves = ((0, half), (half, T))
+        for k, (b, (lo, hi)) in enumerate(((0, halves[0]), (0, halves[1]), (1, halves[0]))):
+            m1, m2 = mul(b, 0, lo, hi), mul(b, 1, lo, hi)
+            add_on_tensor(b, m1[:], m2[:], lo, hi, k % 2, 4 + k % 2)
+        m1, m2 = mul(1, 0, half, T), mul(1, 1, half, T)
+        pending = (1, m1[:], m2[:], half, T)
         m1 = mul(2, 0, 0, T)
         add_on_vector(*pending)
         pending = None

@@ -55,9 +55,8 @@ def tile_moe_rag_mlp_relu_kernel(
         pos2_t = lists.tile([P, T // 16], U16, name="pos2_t")
 
         w1_raw = {e: keep.tile([P, 2 * H], U8, name=f"w1_raw{e}", align_bytes=64)[:] for e in order[1:]}
-        held = S - CH
-        first_raw = early.tile([P, 3 * H], U8, name="first_raw", offset=4 * held - 64, align_bytes=64)
-        w1s_first, w1_raw[FIRST] = first_raw[:, 0:H], first_raw[:, H : 3 * H]
+        w1_raw[FIRST] = early.tile([P, 2 * H], U8, name="first_raw", offset=4 * S - H, align_bytes=64)[:]
+        w1s_first = keep.tile([P, H], U8, name="late", align_bytes=64)[:]
         w1s_raw = keep.tile([P, E - 1, H], U8, name="w1s_raw", align_bytes=64)
         w2_codes = keep.tile([P, E, 2 * N], U8, name="w2_codes", align_bytes=64)
         w2s = keep.tile([P, E, N], U8, name="w2s", align_bytes=64)
@@ -80,11 +79,11 @@ def tile_moe_rag_mlp_relu_kernel(
         for c, w in enumerate(XW):
             nc.sync.dma_start(out=x_raw[c][:], in_=xT[:, X0[c] : X0[c] + w].rearrange("(p j) w -> p j w", j=PACK))
         load_w1(order[0])
-        nc.sync.dma_start(offs_t[:], offs)
         for q in range(4):
             nc.sync.dma_start(
                 out=w1s_first[32 * q : 32 * q + 4].bitcast(I32), in_=w1_scales[FIRST, 0, 4 * q : 4 * q + 4, :].bitcast(I32)
             )
+        nc.sync.dma_start(offs_t[:], offs)
         load_w1(order[1])
         for q in range(4):
             nc.sync.dma_start(
@@ -127,11 +126,11 @@ def tile_moe_rag_mlp_relu_kernel(
         x_quant(len(XW) - 1)
 
         w1_codes, w1s = {}, {}
-        late = early.tile([P, (E - 1) * 3 * H], U8, name="late", offset=5 * held, align_bytes=64)
+        late = keep.tile([P, (E - 1) * 3 * H], U8, name="late", align_bytes=64)
         for i, e in enumerate(order):
             if i == 0:
                 engine, raw_scales = nc.vector, w1s_first
-                both = keep.tile([P, 3 * H], U8, name="w1_first", align_bytes=64)[:]
+                both = keep.tile([P, 3 * H], U8, name=f"x_raw{len(XW) - 1}", align_bytes=64)[:]
             else:
                 engine, raw_scales = nc.gpsimd, w1s_raw[:, e, :]
                 both = late[:, (i - 1) * 3 * H : i * 3 * H]
@@ -150,15 +149,11 @@ def tile_moe_rag_mlp_relu_kernel(
         def bank(k):
             return psum.tile([P, PACK, CH], F32, name=f"bank{k}", bufs=1)
 
-        first_words = keep.tile([P, CH], U32, name="first_words", align_bytes=64)
-        first_bytes = keep.tile([P, CH], U8, name="first_bytes", align_bytes=64)
-        held_words = early.tile([P, held], U32, name="held_words", offset=0, align_bytes=64)
-        held_bytes = early.tile([P, held], U8, name="held_bytes", offset=4 * held, align_bytes=64)
+        slot_words = early.tile([P, S], U32, name="slot_words", offset=0, align_bytes=64)
+        slot_bytes = early.tile([P, S], U8, name="slot_bytes", offset=4 * S, align_bytes=64)
 
         def gathered(lo, hi):
-            if lo * CH == held:
-                return first_words[:], first_bytes[:]
-            return held_words[:, lo * CH : hi * CH], held_bytes[:, lo * CH : hi * CH]
+            return slot_words[:, lo * CH : hi * CH], slot_bytes[:, lo * CH : hi * CH]
 
         for lo, hi in pieces:
             words, bytes_ = gathered(lo, hi)
@@ -193,7 +188,7 @@ def tile_moe_rag_mlp_relu_kernel(
             else:
                 nc.scalar.activation(o, a, RELU)
 
-        for run in ((11,), (10,), (9,), (8, 7), (6, 5), (4,), (3,), (2,), (1, 0)):
+        for run in ((11,), (10,), (9,), (8,), (7,), (6, 5), (4,), (3,), (2,), (1, 0)):
             sums = [(c, layer1(c)) for c in run]
             for c, acc in reversed(sums):
                 relu(c, acc)

@@ -227,9 +227,8 @@ def tile_moe_rag_mlp_relu_kernel(
 
         for lo, hi, k, engine in ((8, 12, 0, "S"), (4, 8, 1, "S"), (2, 4, 2, "V"), (0, 2, 7, "V")):
             layer2(0, lo, hi, k, engine)
-        for b in (1, 2):
-            for k in range(3):
-                layer2(b, 8 - 4 * k, 12 - 4 * k, (0, 1, 3)[k], "S")
+        for k in range(3):
+            layer2(1, 8 - 4 * k, 12 - 4 * k, (0, 1, 3)[k], "S")
 
         def mul(b, r, lo, hi):
             g = keep.tile([P, hi - lo], F32, name=f"m{b}_{r}_{lo}", align_bytes=64)
@@ -242,9 +241,10 @@ def tile_moe_rag_mlp_relu_kernel(
             nc.vector.tensor_tensor(o[:], m1, m2, ADD)
             nc.sync.dma_start(out=out[b * P : (b + 1) * P, lo:hi], in_=o[:])
 
-        def add_on_tensor(b, m1, m2, lo, hi, bank_turned, bank_back):
+        def turn_and_add(b, lo, hi, k):
+            m1, m2 = mul(b, 0, lo, hi), mul(b, 1, lo, hi)
             n = (hi - lo) // P
-            turned = bank(bank_turned)
+            turned = bank(k)
             for c in range(n):
                 for r, m in enumerate((m1, m2)):
                     nc.tensor.matmul(
@@ -252,26 +252,36 @@ def tile_moe_rag_mlp_relu_kernel(
                     )
             z = keep.tile([P, n, P], F32, name=f"z{b}_{lo}", align_bytes=64)
             nc.scalar.copy(z[:], turned[:, 0:n, :])
-            back = bank(bank_back)
+            return b, lo, hi, z
+
+        def turn_back(b, lo, hi, z, k, queue):
+            n = (hi - lo) // P
+            back = bank(k)
             for c in range(n):
                 nc.tensor.transpose(back[:, c, :], z[:, c, :], ident[:])
             o = keep.tile([P, n, P], F32, name=f"o{b}_{lo}", align_bytes=64)
             nc.scalar.copy(o[:], back[:, 0:n, :])
-            nc.scalar.dma_start(out=out[b * P : (b + 1) * P, lo:hi], in_=o[:].rearrange("p c t -> p (c t)"))
+            queue.dma_start(out=out[b * P : (b + 1) * P, lo:hi], in_=o[:].rearrange("p c t -> p (c t)"))
+
+        def on_vector(b, first, parts):
+            m1 = mul(b, 0, first, T)
+            pending = None
+            for lo, hi in parts:
+                m2 = mul(b, 1, lo, hi)
+                if pending is not None:
+                    add_on_vector(*pending)
+                pending = (b, m1[:, lo - first : hi - first], m2[:], lo, hi)
+            add_on_vector(*pending)
 
         half = T // 2
-        halves = ((0, half), (half, T))
-        for k, (b, (lo, hi)) in enumerate(((0, halves[0]), (0, halves[1]), (1, halves[0]))):
-            m1, m2 = mul(b, 0, lo, hi), mul(b, 1, lo, hi)
-            add_on_tensor(b, m1[:], m2[:], lo, hi, k % 2, 4 + k % 2)
-        m1, m2 = mul(1, 0, half, T), mul(1, 1, half, T)
-        pending = (1, m1[:], m2[:], half, T)
-        m1 = mul(2, 0, 0, T)
-        add_on_vector(*pending)
-        pending = None
-        for lo, hi in ((0, 384), (384, 640), (640, T)):
-            m2 = mul(2, 1, lo, hi)
-            if pending is not None:
-                add_on_vector(*pending)
-            pending = (2, m1[:, lo:hi], m2[:], lo, hi)
-        add_on_vector(*pending)
+        layer2(2, 8, 12, 0, "S")
+        first = turn_and_add(0, 0, half, 1)
+        layer2(2, 4, 8, 3, "S")
+        second = turn_and_add(0, half, T, 0)
+        layer2(2, 0, 4, 1, "S")
+        turn_back(*first, 4, nc.sync)
+        third = turn_and_add(1, 0, 384, 0)
+        turn_back(*second, 5, nc.scalar)
+        turn_back(*third, 6, nc.scalar)
+        on_vector(1, 384, ((384, 640), (640, T)))
+        on_vector(2, 0, ((0, 384), (384, 640), (640, T)))

@@ -5,16 +5,20 @@ from concourse.masks import make_identity
 
 K, T, E, H, N = 512, 768, 4, 512, 384
 COUNTS = (256, 384, 512, 384)
-STARTS = (0, 256, 640, 1152)
-S = 1536
+S = sum(COUNTS)
 P = 128
 PACK = 4
 CH = 128
-XW = (384, 256, 128)
-X0 = (0, 384, 640)
-X_VECTOR = (208, 160, 80)
-FIRST = 3
+CHUNKS = S // CH
+BANKS = 8
+LIST = 16
 FLOPS = 2 * S * (K * H + H * N)
+
+X_TOKENS = (384, 256, 128)
+X_ON_VECTOR = (256, 112, 96)
+GATHER_CHUNKS = (1, 2, 3, 3, 3)
+GROUP_CHUNKS = (4, 4, 2, 1, 1)
+RELU_ON_VECTOR = (4, 2)
 
 F32 = mybir.dt.float32
 BF16 = mybir.dt.bfloat16
@@ -30,258 +34,259 @@ MULT = mybir.AluOpType.mult
 ADD = mybir.AluOpType.add
 
 
-def widths(n):
-    runs, lo = [], 0
-    for w in (512, 256, 128):
-        while n - lo >= w:
-            runs.append((lo, lo + w))
-            lo = lo + w
-    return runs
+def runs(n):
+    cut, lo = [], 0
+    for width in (512, 256, 128):
+        while n - lo >= width:
+            cut.append((lo, lo + width))
+            lo = lo + width
+    return cut
+
+
+def from_the_end(sizes):
+    ranges, hi = [], CHUNKS
+    for size in sizes:
+        ranges.append((hi - size, hi))
+        hi = hi - size
+    return ranges
 
 
 def tile_moe_rag_mlp_relu_kernel(
     tc, xT, w1_words, w1_scales, w2_words, w2_scales, gate, offs, pos1, pos2, out
 ):
     nc = tc.nc
-    order = [FIRST - i for i in range(E)]
+    order = list(reversed(range(E)))
+    lead = order[0]
+    x_first = [sum(X_TOKENS[:c]) for c in range(len(X_TOKENS))]
+    x_last = len(X_TOKENS) - 1
+    expert = [e for e in range(E) for s in range(0, COUNTS[e], CH)]
+    groups = from_the_end(GROUP_CHUNKS)
+
     with ExitStack() as ctx:
         lists = ctx.enter_context(tc.tile_pool(name="lists", bufs=1))
         keep = ctx.enter_context(tc.tile_pool(name="keep", bufs=1))
-        early = ctx.enter_context(tc.tile_pool(name="early", bufs=1))
+        placed = ctx.enter_context(tc.tile_pool(name="placed", bufs=1))
         psum = ctx.enter_context(tc.psum_pool(name="psum", bufs=1))
 
-        offs_t = lists.tile([P, 2 * T // 16], U16, name="offs_t")
-        pos1_t = lists.tile([P, T // 16], U16, name="pos1_t")
-        pos2_t = lists.tile([P, T // 16], U16, name="pos2_t")
+        offs_t = lists.tile([P, S // LIST], U16, name="offs_t")
+        pos1_t = lists.tile([P, T // LIST], U16, name="pos1_t")
+        pos2_t = lists.tile([P, T // LIST], U16, name="pos2_t")
 
         w1_raw = {e: keep.tile([P, 2 * H], U8, name=f"w1_raw{e}", align_bytes=64)[:] for e in order[1:]}
-        w1_raw[FIRST] = early.tile([P, 2 * H], U8, name="first_raw", offset=4 * S - H, align_bytes=64)[:]
-        w1s_first = keep.tile([P, H], U8, name="late", align_bytes=64)[:]
-        w1s_raw = keep.tile([P, E - 1, H], U8, name="w1s_raw", align_bytes=64)
+        w1_raw[lead] = placed.tile([P, 2 * H], U8, name="w1_raw_lead", offset=4 * S - H, align_bytes=64)[:]
+        w1s_raw_lead = keep.tile([P, H], U8, name="lead_scales_then_w1_rest", align_bytes=64)[:]
+        w1s_raw_rest = keep.tile([P, E - 1, H], U8, name="w1s_raw_rest", align_bytes=64)
         w2_codes = keep.tile([P, E, 2 * N], U8, name="w2_codes", align_bytes=64)
         w2s = keep.tile([P, E, N], U8, name="w2s", align_bytes=64)
-        x_raw = [keep.tile([P, PACK, w], F32, name=f"x_raw{c}", align_bytes=64) for c, w in enumerate(XW)]
+        x_raw = [keep.tile([P, PACK, w], F32, name=f"x_raw{c}", align_bytes=64) for c, w in enumerate(X_TOKENS)]
         x_scales = keep.tile([P, T], U8, name="x_scales", align_bytes=64)
         gates = keep.tile([P, 2, T], F32, name="gates", align_bytes=64)
         ident = keep.tile([P, P], F32, name="ident", align_bytes=64)
-        ys = [keep.tile([P, S], F32, name=f"y{b}", align_bytes=64) for b in range(3)]
+        ys = [keep.tile([P, S], F32, name=f"y{b}", align_bytes=64) for b in range(N // P)]
 
-        nc.vector.memset(w1s_first.bitcast(I32), 0)
-        nc.vector.memset(w1s_raw[:].rearrange("p e n -> p (e n)").bitcast(I32), 0)
+        nc.vector.memset(w1s_raw_lead.bitcast(I32), 0)
+        nc.vector.memset(w1s_raw_rest[:].rearrange("p e n -> p (e n)").bitcast(I32), 0)
         nc.vector.memset(ident[:], 0.0)
         make_identity(nc, ident[:], nomemset=True)
         nc.vector.memset(x_scales[:].bitcast(I32), 0)
         nc.vector.memset(w2s[:].rearrange("p e n -> p (e n)").bitcast(I32), 0)
 
-        def load_w1(e):
+        def load_w1_words(e):
             nc.sync.dma_start(out=w1_raw[e].bitcast(I32), in_=w1_words[e, 0].bitcast(I32))
 
-        for c, w in enumerate(XW):
-            nc.sync.dma_start(out=x_raw[c][:], in_=xT[:, X0[c] : X0[c] + w].rearrange("(p j) w -> p j w", j=PACK))
-        load_w1(order[0])
-        for q in range(4):
-            nc.sync.dma_start(
-                out=w1s_first[32 * q : 32 * q + 4].bitcast(I32), in_=w1_scales[FIRST, 0, 4 * q : 4 * q + 4, :].bitcast(I32)
-            )
+        def load_scale_rows(tile, rows):
+            for q in range(4):
+                nc.sync.dma_start(out=tile[32 * q : 32 * q + 4].bitcast(I32), in_=rows[4 * q : 4 * q + 4].bitcast(I32))
+
+        for c, w in enumerate(X_TOKENS):
+            rows = xT[:, x_first[c] : x_first[c] + w]
+            nc.sync.dma_start(out=x_raw[c][:], in_=rows.rearrange("(p j) w -> p j w", j=PACK))
+        load_w1_words(lead)
+        load_scale_rows(w1s_raw_lead, w1_scales[lead, 0])
         nc.sync.dma_start(offs_t[:], offs)
-        load_w1(order[1])
-        for q in range(4):
-            nc.sync.dma_start(
-                out=w1s_raw[32 * q : 32 * q + 4].bitcast(I32),
-                in_=w1_scales[0 : E - 1, 0, 4 * q : 4 * q + 4, :].rearrange("e q n -> q e n").bitcast(I32),
-            )
-        load_w1(order[2])
-        load_w1(order[3])
+        load_w1_words(order[1])
+        load_scale_rows(w1s_raw_rest, w1_scales[0:lead, 0].rearrange("e q n -> q e n"))
+        load_w1_words(order[2])
+        load_w1_words(order[3])
         nc.sync.dma_start(out=w2_codes[:].bitcast(I32), in_=w2_words[:, 0].rearrange("e p b -> p e b").bitcast(I32))
-        for q in range(4):
-            nc.sync.dma_start(
-                out=w2s[32 * q : 32 * q + 4].bitcast(I32),
-                in_=w2_scales[:, 0, 4 * q : 4 * q + 4, :].rearrange("e q n -> q e n").bitcast(I32),
-            )
+        load_scale_rows(w2s, w2_scales[:, 0].rearrange("e q n -> q e n"))
         nc.sync.dma_start(pos1_t[:], pos1)
         nc.sync.dma_start(pos2_t[:], pos2)
         nc.sync.dma_start(out=gates[:], in_=gate[:, 0:P, :].rearrange("g p t -> p g t"))
 
         x_codes = keep.tile([P, T], U32, name="x_codes", align_bytes=64)
-        x_grp = [keep.tile([P, w, PACK], BF16, name=f"x_grp{c}", align_bytes=64) for c, w in enumerate(XW)]
+        x_bf16 = [keep.tile([P, w, PACK], BF16, name=f"x_bf16{c}", align_bytes=64) for c, w in enumerate(X_TOKENS)]
 
-        def x_quant(c):
-            for lo, hi in widths(XW[c]):
+        def quantise_tokens(c):
+            for lo, hi in runs(X_TOKENS[c]):
                 nc.vector.quantize_mx(
-                    out=x_codes[:, X0[c] + lo : X0[c] + hi].bitcast(FP8X4),
-                    scales=x_scales[:, X0[c] + lo : X0[c] + hi],
-                    in_=x_grp[c][:, lo:hi, :].rearrange("p w j -> p (w j)"),
+                    out=x_codes[:, x_first[c] + lo : x_first[c] + hi].bitcast(FP8X4),
+                    scales=x_scales[:, x_first[c] + lo : x_first[c] + hi],
+                    in_=x_bf16[c][:, lo:hi, :].rearrange("p w j -> p (w j)"),
                 )
 
-        def interleave(c, lo, hi):
-            o = x_grp[c][:, lo:hi, :].rearrange("p (c i) t -> p c t i", i=4)
-            i = x_raw[c][:, :, lo:hi].rearrange("p t (c i) -> p c t i", i=4)
-            return o, i
+        def interleaving(c, lo, hi):
+            dst = x_bf16[c][:, lo:hi, :].rearrange("p (c i) t -> p c t i", i=4)
+            src = x_raw[c][:, :, lo:hi].rearrange("p t (c i) -> p c t i", i=4)
+            return dst, src
 
-        for c, w in enumerate(XW):
-            nc.vector.tensor_copy(*interleave(c, 0, X_VECTOR[c]))
-            nc.scalar.activation(*interleave(c, X_VECTOR[c], w), COPY)
+        for c, w in enumerate(X_TOKENS):
+            nc.vector.tensor_copy(*interleaving(c, 0, X_ON_VECTOR[c]))
+            nc.scalar.activation(*interleaving(c, X_ON_VECTOR[c], w), COPY)
             if c > 0:
-                x_quant(c - 1)
-        x_quant(len(XW) - 1)
+                quantise_tokens(c - 1)
+        quantise_tokens(x_last)
 
         w1_codes, w1s = {}, {}
-        late = keep.tile([P, (E - 1) * 3 * H], U8, name="late", align_bytes=64)
+        w1_rest = keep.tile([P, (E - 1) * 3 * H], U8, name="lead_scales_then_w1_rest", align_bytes=64)
         for i, e in enumerate(order):
-            if i == 0:
-                engine, raw_scales = nc.vector, w1s_first
-                both = keep.tile([P, 3 * H], U8, name=f"x_raw{len(XW) - 1}", align_bytes=64)[:]
+            if e == lead:
+                engine, raw_scales = nc.vector, w1s_raw_lead
+                permuted = keep.tile([P, 3 * H], U8, name=f"x_raw{x_last}", align_bytes=64)[:]
             else:
-                engine, raw_scales = nc.gpsimd, w1s_raw[:, e, :]
-                both = late[:, (i - 1) * 3 * H : i * 3 * H]
-            w1_codes[e], w1s[e] = both[:, 0 : 2 * H], both[:, 2 * H : 3 * H]
+                engine, raw_scales = nc.gpsimd, w1s_raw_rest[:, e, :]
+                permuted = w1_rest[:, (i - 1) * 3 * H : i * 3 * H]
+            w1_codes[e], w1s[e] = permuted[:, 0 : 2 * H], permuted[:, 2 * H : 3 * H]
             engine.tensor_copy(
                 w1_codes[e].bitcast(U16).rearrange("p (t m) -> p t m", t=PACK),
                 w1_raw[e].bitcast(U16).rearrange("p (m t) -> p t m", t=PACK),
             )
-            engine.tensor_copy(w1s[e].rearrange("p (t m) -> p t m", t=PACK), raw_scales.rearrange("p (m t) -> p t m", t=PACK))
+            engine.tensor_copy(
+                w1s[e].rearrange("p (t m) -> p t m", t=PACK), raw_scales.rearrange("p (m t) -> p t m", t=PACK)
+            )
 
-        expert = [e for e in range(E) for s in range(0, COUNTS[e], CH)]
-        groups = ((8, 12), (4, 8), (2, 4), (0, 2))
-        vector_chunks = (4, 2)
-        pieces = ((11, 12), (9, 11), (6, 9), (3, 6), (0, 3))
+        slot_words = placed.tile([P, S], U32, name="slot_words", offset=0, align_bytes=64)
+        slot_bytes = placed.tile([P, S], U8, name="slot_bytes", offset=4 * S, align_bytes=64)
+        for lo, hi in from_the_end(GATHER_CHUNKS):
+            entries = offs_t[:, lo * CH // LIST : hi * CH // LIST]
+            nc.vector.tensor_copy(slot_words[:, lo * CH : hi * CH], x_codes[:].indirect(entries))
+            nc.vector.tensor_copy(slot_bytes[:, lo * CH : hi * CH], x_scales[:].indirect(entries))
 
         def bank(k):
             return psum.tile([P, PACK, CH], F32, name=f"bank{k}", bufs=1)
 
-        slot_words = early.tile([P, S], U32, name="slot_words", offset=0, align_bytes=64)
-        slot_bytes = early.tile([P, S], U8, name="slot_bytes", offset=4 * S, align_bytes=64)
+        def bank_of(c):
+            return (CHUNKS - 1 - c) % BANKS
 
-        def gathered(lo, hi):
-            return slot_words[:, lo * CH : hi * CH], slot_bytes[:, lo * CH : hi * CH]
-
-        for lo, hi in pieces:
-            words, bytes_ = gathered(lo, hi)
-            cols = slice(lo * CH // 16, hi * CH // 16)
-            nc.vector.tensor_copy(words, x_codes[:].indirect(offs_t[:, cols]))
-            nc.vector.tensor_copy(bytes_, x_scales[:].indirect(offs_t[:, cols]))
-
-        h_grp = {lo: keep.tile([P, (hi - lo) * CH, PACK], BF16, name=f"h_grp{lo}", align_bytes=64) for lo, hi in groups}
-
-        def layer1(c):
-            e = expert[c]
-            words, bytes_ = gathered(c, c + 1)
-            acc = bank((len(expert) - 1 - c) % 8)
-            for t in range(PACK):
-                nc.tensor.matmul_mx(
-                    out=acc[:, t, :],
-                    lhsT=w1_codes[e][:, 256 * t : 256 * t + 256].bitcast(FP4X4),
-                    lhsT_scale=w1s[e][:, 128 * t : 128 * t + 128],
-                    rhs=words.bitcast(FP8X4),
-                    rhs_scale=bytes_,
-                    start=True,
-                    stop=True,
-                )
-            return acc
-
-        def relu(c, acc):
-            g = max(g for g, g_end in groups if g <= c)
-            o = h_grp[g][:, (c - g) * CH : (c - g + 1) * CH, :]
-            a = acc[:].rearrange("p t n -> p n t")
-            if c in vector_chunks:
-                nc.vector.tensor_scalar_max(o, a, 0.0)
-            else:
-                nc.scalar.activation(o, a, RELU)
-
-        for run in ((11,), (10,), (9,), (8,), (7,), (6, 5), (4,), (3,), (2,), (1, 0)):
-            sums = [(c, layer1(c)) for c in run]
-            for c, acc in reversed(sums):
-                relu(c, acc)
+        h_bf16 = {lo: keep.tile([P, (hi - lo) * CH, PACK], BF16, name=f"h_bf16{lo}", align_bytes=64) for lo, hi in groups}
+        for g, g_end in groups:
+            for c in reversed(range(g, g_end)):
+                e = expert[c]
+                sums = bank(bank_of(c))
+                for t in range(PACK):
+                    nc.tensor.matmul_mx(
+                        out=sums[:, t, :],
+                        lhsT=w1_codes[e][:, 2 * P * t : 2 * P * (t + 1)].bitcast(FP4X4),
+                        lhsT_scale=w1s[e][:, P * t : P * (t + 1)],
+                        rhs=slot_words[:, c * CH : (c + 1) * CH].bitcast(FP8X4),
+                        rhs_scale=slot_bytes[:, c * CH : (c + 1) * CH],
+                        start=True,
+                        stop=True,
+                    )
+                dst = h_bf16[g][:, (c - g) * CH : (c - g + 1) * CH, :]
+                src = sums[:].rearrange("p t n -> p n t")
+                if c in RELU_ON_VECTOR:
+                    nc.vector.tensor_scalar_max(dst, src, 0.0)
+                else:
+                    nc.scalar.activation(dst, src, RELU)
 
         h_codes, h_scales = {}, {}
-        for lo, hi in groups:
-            h_codes[lo] = keep.tile([P, (hi - lo) * CH], U32, name=f"h_codes{lo}", align_bytes=64)
-            h_scales[lo] = keep.tile([P, (hi - lo) * CH], U8, name=f"h_scales{lo}", align_bytes=64)
+        for g, g_end in groups:
+            h_codes[g] = keep.tile([P, (g_end - g) * CH], U32, name=f"h_codes{g}", align_bytes=64)
+            h_scales[g] = keep.tile([P, (g_end - g) * CH], U8, name=f"h_scales{g}", align_bytes=64)
             nc.vector.quantize_mx(
-                out=h_codes[lo][:].bitcast(FP8X4),
-                scales=h_scales[lo][:],
-                in_=h_grp[lo][:].rearrange("p n t -> p (n t)"),
+                out=h_codes[g][:].bitcast(FP8X4),
+                scales=h_scales[g][:],
+                in_=h_bf16[g][:].rearrange("p n t -> p (n t)"),
             )
 
-        def layer2(b, first, last, k, engine):
+        def layer2(b, chunks, k, copy):
+            first, last = chunks
             flat = bank(k)[:].rearrange("p t n -> p (t n)")
             for g, g_end in groups:
                 for e in order:
-                    cs = [c for c in range(max(first, g), min(last, g_end)) if expert[c] == e]
-                    for lo, hi in widths(len(cs) * CH):
-                        cols = slice((cs[0] - g) * CH + lo, (cs[0] - g) * CH + hi)
+                    mine = [c for c in range(max(first, g), min(last, g_end)) if expert[c] == e]
+                    for lo, hi in runs(len(mine) * CH):
+                        in_group = slice((mine[0] - g) * CH + lo, (mine[0] - g) * CH + hi)
                         nc.tensor.matmul_mx(
-                            out=flat[:, (cs[0] - first) * CH + lo : (cs[0] - first) * CH + hi],
-                            lhsT=w2_codes[:, e, 256 * b : 256 * b + 256].bitcast(FP4X4),
-                            lhsT_scale=w2s[:, e, 128 * b : 128 * b + 128],
-                            rhs=h_codes[g][:, cols].bitcast(FP8X4),
-                            rhs_scale=h_scales[g][:, cols],
+                            out=flat[:, (mine[0] - first) * CH + lo : (mine[0] - first) * CH + hi],
+                            lhsT=w2_codes[:, e, 2 * P * b : 2 * P * (b + 1)].bitcast(FP4X4),
+                            lhsT_scale=w2s[:, e, P * b : P * (b + 1)],
+                            rhs=h_codes[g][:, in_group].bitcast(FP8X4),
+                            rhs_scale=h_scales[g][:, in_group],
                             start=True,
                             stop=True,
                         )
-            o, i = ys[b][:, first * CH : last * CH], flat[:, 0 : (last - first) * CH]
-            if engine == "S":
-                nc.scalar.copy(o, i)
-            else:
-                nc.vector.tensor_copy(o, i)
+            copy(ys[b][:, first * CH : last * CH], flat[:, 0 : (last - first) * CH])
 
-        for lo, hi, k, engine in ((8, 12, 0, "S"), (4, 8, 1, "S"), (2, 4, 2, "V"), (0, 2, 7, "V")):
-            layer2(0, lo, hi, k, engine)
-        for k in range(3):
-            layer2(1, 8 - 4 * k, 12 - 4 * k, (0, 1, 3)[k], "S")
+        high, middle, low = from_the_end((PACK, PACK, PACK))
+        bank_a, bank_b, bank_c = bank_of(3), bank_of(2), bank_of(0)
+        layer2(0, high, bank_a, nc.scalar.copy)
+        layer2(0, middle, bank_b, nc.scalar.copy)
+        layer2(0, (1, 4), bank_of(1), nc.vector.tensor_copy)
+        layer2(0, (0, 1), bank_of(4), nc.vector.tensor_copy)
+        layer2(1, high, bank_a, nc.scalar.copy)
+        layer2(1, middle, bank_b, nc.scalar.copy)
+        layer2(1, low, bank_c, nc.scalar.copy)
 
-        def mul(b, r, lo, hi):
-            g = keep.tile([P, hi - lo], F32, name=f"m{b}_{r}_{lo}", align_bytes=64)
-            pos = (pos1_t, pos2_t)[r]
-            nc.vector.tensor_tensor(g[:], ys[b][:].indirect(pos[:, lo // 16 : hi // 16]), gates[:, r, lo:hi], MULT)
-            return g
-
-        def add_on_vector(b, m1, m2, lo, hi):
-            o = keep.tile([P, hi - lo], F32, name=f"o{b}_{lo}", align_bytes=64)
-            nc.vector.tensor_tensor(o[:], m1, m2, ADD)
-            nc.sync.dma_start(out=out[b * P : (b + 1) * P, lo:hi], in_=o[:])
+        def gated(b, r, lo, hi):
+            product = keep.tile([P, hi - lo], F32, name=f"product{b}_{r}_{lo}", align_bytes=64)
+            entries = (pos1_t, pos2_t)[r][:, lo // LIST : hi // LIST]
+            nc.vector.tensor_tensor(product[:], ys[b][:].indirect(entries), gates[:, r, lo:hi], MULT)
+            return product
 
         def turn_and_add(b, lo, hi, k):
-            m1, m2 = mul(b, 0, lo, hi), mul(b, 1, lo, hi)
+            products = gated(b, 0, lo, hi), gated(b, 1, lo, hi)
             n = (hi - lo) // P
             turned = bank(k)
             for c in range(n):
-                for r, m in enumerate((m1, m2)):
+                for r, product in enumerate(products):
                     nc.tensor.matmul(
-                        turned[:, c, :], m[:, c * P : (c + 1) * P], ident[:], start=r == 0, stop=r == 1, is_transpose=True
+                        turned[:, c, :],
+                        product[:, c * P : (c + 1) * P],
+                        ident[:],
+                        start=r == 0,
+                        stop=r == 1,
+                        is_transpose=True,
                     )
-            z = keep.tile([P, n, P], F32, name=f"z{b}_{lo}", align_bytes=64)
-            nc.scalar.copy(z[:], turned[:, 0:n, :])
-            return b, lo, hi, z
+            total = keep.tile([P, n, P], F32, name=f"turned{b}_{lo}", align_bytes=64)
+            nc.scalar.copy(total[:], turned[:, 0:n, :])
+            return b, lo, hi, total
 
-        def turn_back(b, lo, hi, z, k, queue):
+        def turn_back_and_store(b, lo, hi, total, k, queue):
             n = (hi - lo) // P
             back = bank(k)
             for c in range(n):
-                nc.tensor.transpose(back[:, c, :], z[:, c, :], ident[:])
-            o = keep.tile([P, n, P], F32, name=f"o{b}_{lo}", align_bytes=64)
-            nc.scalar.copy(o[:], back[:, 0:n, :])
-            queue.dma_start(out=out[b * P : (b + 1) * P, lo:hi], in_=o[:].rearrange("p c t -> p (c t)"))
+                nc.tensor.transpose(back[:, c, :], total[:, c, :], ident[:])
+            result = keep.tile([P, n, P], F32, name=f"result{b}_{lo}", align_bytes=64)
+            nc.scalar.copy(result[:], back[:, 0:n, :])
+            queue.dma_start(out=out[b * P : (b + 1) * P, lo:hi], in_=result[:].rearrange("p c t -> p (c t)"))
 
-        def on_vector(b, first, parts):
-            m1 = mul(b, 0, first, T)
-            pending = None
-            for lo, hi in parts:
-                m2 = mul(b, 1, lo, hi)
-                if pending is not None:
-                    add_on_vector(*pending)
-                pending = (b, m1[:, lo - first : hi - first], m2[:], lo, hi)
-            add_on_vector(*pending)
+        def add_and_store(b, first_product, second_product, lo, hi):
+            result = keep.tile([P, hi - lo], F32, name=f"result{b}_{lo}", align_bytes=64)
+            nc.vector.tensor_tensor(result[:], first_product, second_product, ADD)
+            nc.sync.dma_start(out=out[b * P : (b + 1) * P, lo:hi], in_=result[:])
+
+        def combine_on_vector(b, cuts):
+            first_product = gated(b, 0, cuts[0], cuts[-1])
+            waiting = None
+            for lo, hi in zip(cuts[:-1], cuts[1:]):
+                second_product = gated(b, 1, lo, hi)
+                if waiting is not None:
+                    add_and_store(*waiting)
+                waiting = (b, first_product[:, lo - cuts[0] : hi - cuts[0]], second_product[:], lo, hi)
+            add_and_store(*waiting)
 
         half = T // 2
-        layer2(2, 8, 12, 0, "S")
-        first = turn_and_add(0, 0, half, 1)
-        layer2(2, 4, 8, 3, "S")
-        second = turn_and_add(0, half, T, 0)
-        layer2(2, 0, 4, 1, "S")
-        turn_back(*first, 4, nc.sync)
-        third = turn_and_add(1, 0, 384, 0)
-        turn_back(*second, 5, nc.scalar)
-        turn_back(*third, 6, nc.scalar)
-        on_vector(1, 384, ((384, 640), (640, T)))
-        on_vector(2, 0, ((0, 384), (384, 640), (640, T)))
+        back_banks = [bank_of(c) for c in (7, 6, 5)]
+        layer2(2, high, bank_a, nc.scalar.copy)
+        first_half = turn_and_add(0, 0, half, bank_b)
+        layer2(2, middle, bank_c, nc.scalar.copy)
+        second_half = turn_and_add(0, half, T, bank_a)
+        layer2(2, low, bank_b, nc.scalar.copy)
+        turn_back_and_store(*first_half, back_banks[0], nc.sync)
+        third_half = turn_and_add(1, 0, half, bank_a)
+        turn_back_and_store(*second_half, back_banks[1], nc.scalar)
+        turn_back_and_store(*third_half, back_banks[2], nc.scalar)
+        combine_on_vector(1, (half, T - P, T))
+        combine_on_vector(2, (0, half, T - P, T))

@@ -65,16 +65,14 @@ def tile_moe_rag_mlp_relu_kernel(
     with ExitStack() as ctx:
         lists = ctx.enter_context(tc.tile_pool(name="lists", bufs=1))
         keep = ctx.enter_context(tc.tile_pool(name="keep", bufs=1))
-        placed = ctx.enter_context(tc.tile_pool(name="placed", bufs=1))
         psum = ctx.enter_context(tc.psum_pool(name="psum", bufs=1))
 
         offs_t = lists.tile([P, S // LIST], U16, name="offs_t")
         pos1_t = lists.tile([P, T // LIST], U16, name="pos1_t")
         pos2_t = lists.tile([P, T // LIST], U16, name="pos2_t")
 
-        w1_raw = {e: keep.tile([P, 2 * H], U8, name=f"w1_raw{e}", align_bytes=64)[:] for e in order[1:]}
-        w1_raw[lead] = placed.tile([P, 2 * H], U8, name="w1_raw_lead", offset=4 * S - H, align_bytes=64)[:]
-        w1s_raw_lead = keep.tile([P, H], U8, name="lead_scales_then_w1_rest", align_bytes=64)[:]
+        w1_raw = {e: keep.tile([P, 2 * H], U8, name=f"w1_raw{e}", align_bytes=64)[:] for e in order}
+        w1s_raw_lead = keep.tile([P, H], U8, name="w1s_raw_lead", align_bytes=64)[:]
         w1s_raw_rest = keep.tile([P, E - 1, H], U8, name="w1s_raw_rest", align_bytes=64)
         w2_codes = keep.tile([P, E, 2 * N], U8, name="w2_codes", align_bytes=64)
         w2s = keep.tile([P, E, N], U8, name="w2s", align_bytes=64)
@@ -98,11 +96,12 @@ def tile_moe_rag_mlp_relu_kernel(
             for q in range(4):
                 nc.sync.dma_start(out=tile[32 * q : 32 * q + 4].bitcast(I32), in_=rows[4 * q : 4 * q + 4].bitcast(I32))
 
-        for c, w in enumerate(X_TOKENS):
-            rows = xT[:, x_first[c] : x_first[c] + w]
-            nc.sync.dma_start(out=x_raw[c][:], in_=rows.rearrange("(p j) w -> p j w", j=PACK))
-        load_w1_words(lead)
+        by_word = xT.rearrange("(p j) w -> p j w", j=PACK)
+        nc.sync.dma_start(out=x_raw[0][:], in_=by_word[:, :, 0 : X_TOKENS[0]])
         load_scale_rows(w1s_raw_lead, w1_scales[lead, 0])
+        for c in range(1, len(X_TOKENS)):
+            nc.sync.dma_start(out=x_raw[c][:], in_=by_word[:, :, x_first[c] : x_first[c] + X_TOKENS[c]])
+        load_w1_words(lead)
         nc.sync.dma_start(offs_t[:], offs)
         load_w1_words(order[1])
         load_scale_rows(w1s_raw_rest, w1_scales[0:lead, 0].rearrange("e q n -> q e n"))
@@ -130,33 +129,29 @@ def tile_moe_rag_mlp_relu_kernel(
             src = x_raw[c][:, :, lo:hi].rearrange("p t (c i) -> p c t i", i=4)
             return dst, src
 
+        def permute(engine, dst, src):
+            engine.tensor_copy(dst.rearrange("p (t m) -> p t m", t=PACK), src.rearrange("p (m t) -> p t m", t=PACK))
+
+        w1s = {lead: keep.tile([P, H], U8, name="w1s_lead", align_bytes=64)[:]}
         for c, w in enumerate(X_TOKENS):
             nc.vector.tensor_copy(*interleaving(c, 0, X_ON_VECTOR[c]))
             nc.scalar.activation(*interleaving(c, X_ON_VECTOR[c], w), COPY)
-            if c > 0:
+            if c == 0:
+                permute(nc.vector, w1s[lead], w1s_raw_lead)
+            else:
                 quantise_tokens(c - 1)
         quantise_tokens(x_last)
 
-        w1_codes, w1s = {}, {}
-        w1_rest = keep.tile([P, (E - 1) * 3 * H], U8, name="lead_scales_then_w1_rest", align_bytes=64)
-        for i, e in enumerate(order):
-            if e == lead:
-                engine, raw_scales = nc.vector, w1s_raw_lead
-                permuted = keep.tile([P, 3 * H], U8, name=f"x_raw{x_last}", align_bytes=64)[:]
-            else:
-                engine, raw_scales = nc.gpsimd, w1s_raw_rest[:, e, :]
-                permuted = w1_rest[:, (i - 1) * 3 * H : i * 3 * H]
-            w1_codes[e], w1s[e] = permuted[:, 0 : 2 * H], permuted[:, 2 * H : 3 * H]
-            engine.tensor_copy(
-                w1_codes[e].bitcast(U16).rearrange("p (t m) -> p t m", t=PACK),
-                w1_raw[e].bitcast(U16).rearrange("p (m t) -> p t m", t=PACK),
-            )
-            engine.tensor_copy(
-                w1s[e].rearrange("p (t m) -> p t m", t=PACK), raw_scales.rearrange("p (m t) -> p t m", t=PACK)
-            )
+        w1_codes = {lead: keep.tile([P, 2 * H], U8, name=f"x_raw{x_last}", align_bytes=64)[:]}
+        permute(nc.vector, w1_codes[lead].bitcast(U16), w1_raw[lead].bitcast(U16))
+        w1_rest = keep.tile([P, E - 1, 3 * H], U8, name=f"w1_raw{lead}", align_bytes=64)
+        for i, e in enumerate(order[1:]):
+            w1_codes[e], w1s[e] = w1_rest[:, i, 0 : 2 * H], w1_rest[:, i, 2 * H : 3 * H]
+            permute(nc.gpsimd, w1_codes[e].bitcast(U16), w1_raw[e].bitcast(U16))
+            permute(nc.gpsimd, w1s[e], w1s_raw_rest[:, e, :])
 
-        slot_words = placed.tile([P, S], U32, name="slot_words", offset=0, align_bytes=64)
-        slot_bytes = placed.tile([P, S], U8, name="slot_bytes", offset=4 * S, align_bytes=64)
+        slot_words = keep.tile([P, S], U32, name="slot_words", align_bytes=64)
+        slot_bytes = keep.tile([P, S], U8, name="slot_bytes", align_bytes=64)
         for lo, hi in from_the_end(GATHER_CHUNKS):
             entries = offs_t[:, lo * CH // LIST : hi * CH // LIST]
             nc.vector.tensor_copy(slot_words[:, lo * CH : hi * CH], x_codes[:].indirect(entries))

@@ -15,7 +15,7 @@ LIST = 16
 FLOPS = 2 * S * (K * H + H * N)
 
 X_TOKENS = (384, 256, 128)
-X_ON_VECTOR = (256, 112, 96)
+X_ON_VECTOR = (192, 112, 80)
 GATHER_CHUNKS = (1, 2, 3, 3, 3)
 GROUP_CHUNKS = (4, 4, 2, 1, 1)
 RELU_ON_VECTOR = (4, 2)
@@ -117,7 +117,7 @@ def tile_moe_rag_mlp_relu_kernel(
         x_bf16 = [keep.tile([P, w, PACK], BF16, name=f"x_bf16{c}", align_bytes=64) for c, w in enumerate(X_TOKENS)]
 
         def quantise_tokens(c):
-            for lo, hi in runs(X_TOKENS[c]):
+            for lo, hi in ((0, CH), (CH, X_TOKENS[c])) if c == 0 else runs(X_TOKENS[c]):
                 nc.vector.quantize_mx(
                     out=x_codes[:, x_first[c] + lo : x_first[c] + hi].bitcast(FP8X4),
                     scales=x_scales[:, x_first[c] + lo : x_first[c] + hi],
@@ -230,8 +230,7 @@ def tile_moe_rag_mlp_relu_kernel(
             nc.vector.tensor_tensor(product[:], ys[b][:].indirect(entries), gates[:, r, lo:hi], MULT)
             return product
 
-        def turn_and_add(b, lo, hi, k):
-            products = gated(b, 0, lo, hi), gated(b, 1, lo, hi)
+        def turn_and_add(b, lo, hi, k, products):
             n = (hi - lo) // P
             turned = bank(k)
             for c in range(n):
@@ -262,8 +261,12 @@ def tile_moe_rag_mlp_relu_kernel(
             nc.vector.tensor_tensor(result[:], first_product, second_product, ADD)
             nc.sync.dma_start(out=out[b * P : (b + 1) * P, lo:hi], in_=result[:])
 
-        def combine_on_vector(b, cuts):
+        def both(b, lo, hi):
+            return gated(b, 0, lo, hi), gated(b, 1, lo, hi)
+
+        def combine_on_vector(b, cuts, waiting):
             first_product = gated(b, 0, cuts[0], cuts[-1])
+            add_and_store(*waiting)
             waiting = None
             for lo, hi in zip(cuts[:-1], cuts[1:]):
                 second_product = gated(b, 1, lo, hi)
@@ -275,13 +278,16 @@ def tile_moe_rag_mlp_relu_kernel(
         half = T // 2
         back_banks = [bank_of(c) for c in (7, 6, 5)]
         layer2(2, high, bank_a, nc.scalar.copy)
-        first_half = turn_and_add(0, 0, half, bank_b)
+        first_half = turn_and_add(0, 0, half, bank_b, both(0, 0, half))
         layer2(2, middle, bank_c, nc.scalar.copy)
-        second_half = turn_and_add(0, half, T, bank_a)
+        second_half = turn_and_add(0, half, T, bank_a, both(0, half, T))
         layer2(2, low, bank_b, nc.scalar.copy)
         turn_back_and_store(*first_half, back_banks[0], nc.sync)
-        third_half = turn_and_add(1, 0, half, bank_a)
+        third_half = turn_and_add(1, 0, half, bank_a, both(1, 0, half))
         turn_back_and_store(*second_half, back_banks[1], nc.scalar)
+        first_rest = gated(1, 0, half, T)
+        rest = (1, first_rest[:, T - P - half :], gated(1, 1, T - P, T)[:], T - P, T)
+        fourth = turn_and_add(1, half, T - P, bank_c, (first_rest, gated(1, 1, half, T - P)))
         turn_back_and_store(*third_half, back_banks[2], nc.scalar)
-        combine_on_vector(1, (half, T - P, T))
-        combine_on_vector(2, (0, half, T - P, T))
+        turn_back_and_store(*fourth, back_banks[0], nc.scalar)
+        combine_on_vector(2, (0, half, T - P, T), rest)

@@ -230,7 +230,8 @@ def tile_moe_rag_mlp_relu_kernel(
             nc.vector.tensor_tensor(product[:], ys[b][:].indirect(entries), gates[:, r, lo:hi], MULT)
             return product
 
-        def turn_and_add(b, lo, hi, k, products):
+        def turn_and_add(b, lo, hi, k):
+            products = gated(b, 0, lo, hi), gated(b, 1, lo, hi)
             n = (hi - lo) // P
             turned = bank(k)
             for c in range(n):
@@ -261,13 +262,11 @@ def tile_moe_rag_mlp_relu_kernel(
             nc.vector.tensor_tensor(result[:], first_product, second_product, ADD)
             nc.sync.dma_start(out=out[b * P : (b + 1) * P, lo:hi], in_=result[:])
 
-        def both(b, lo, hi):
-            return gated(b, 0, lo, hi), gated(b, 1, lo, hi)
-
         def combine_on_vector(b, cuts, waiting):
             first_product = gated(b, 0, cuts[0], cuts[-1])
-            add_and_store(*waiting)
-            waiting = None
+            if waiting is not None:
+                add_and_store(*waiting)
+                waiting = None
             for lo, hi in zip(cuts[:-1], cuts[1:]):
                 second_product = gated(b, 1, lo, hi)
                 if waiting is not None:
@@ -278,16 +277,14 @@ def tile_moe_rag_mlp_relu_kernel(
         half = T // 2
         back_banks = [bank_of(c) for c in (7, 6, 5)]
         layer2(2, high, bank_a, nc.scalar.copy)
-        first_half = turn_and_add(0, 0, half, bank_b, both(0, 0, half))
+        first_half = turn_and_add(0, 0, half, bank_b)
         layer2(2, middle, bank_c, nc.scalar.copy)
-        second_half = turn_and_add(0, half, T, bank_a, both(0, half, T))
+        second_half = turn_and_add(0, half, T, bank_a)
         layer2(2, low, bank_b, nc.scalar.copy)
         turn_back_and_store(*first_half, back_banks[0], nc.sync)
-        third_half = turn_and_add(1, 0, half, bank_a, both(1, 0, half))
+        third_half = turn_and_add(1, 0, half, bank_a)
         turn_back_and_store(*second_half, back_banks[1], nc.scalar)
-        first_rest = gated(1, 0, half, T)
-        rest = (1, first_rest[:, T - P - half :], gated(1, 1, T - P, T)[:], T - P, T)
-        fourth = turn_and_add(1, half, T - P, bank_c, (first_rest, gated(1, 1, half, T - P)))
         turn_back_and_store(*third_half, back_banks[2], nc.scalar)
-        turn_back_and_store(*fourth, back_banks[0], nc.scalar)
-        combine_on_vector(2, (0, half, T - P, T), rest)
+        combine_on_vector(1, (half, T - P, T), None)
+        early = gated(2, 0, 0, half), gated(2, 1, 0, half)
+        combine_on_vector(2, (half, T - P, T), (2, early[0][:], early[1][:], 0, half))

@@ -234,14 +234,14 @@ def tile_moe_rag_mlp_relu_kernel(
             products = gated(b, 0, lo, hi), gated(b, 1, lo, hi)
             n = (hi - lo) // P
             turned = bank(k)
-            for c in range(n):
-                for r, product in enumerate(products):
+            for r, product in enumerate(products):
+                for c in range(n):
                     nc.tensor.matmul(
                         turned[:, c, :],
                         product[:, c * P : (c + 1) * P],
                         ident[:],
-                        start=r == 0,
-                        stop=r == 1,
+                        start=(r, c) == (0, 0),
+                        stop=(r, c) == (1, n - 1),
                         is_transpose=True,
                     )
             total = keep.tile([P, n, P], F32, name=f"turned{b}_{lo}", align_bytes=64)
@@ -282,7 +282,7 @@ def tile_moe_rag_mlp_relu_kernel(
         second_half = turn_and_add(0, half, T, bank_a)
         layer2(2, low, bank_b, nc.scalar.copy)
         turn_back_and_store(*first_half, back_banks[0], nc.sync)
-        third_half = turn_and_add(1, 0, half, bank_a)
+        third_half = turn_and_add(1, 0, half, bank_c)
         turn_back_and_store(*second_half, back_banks[1], nc.scalar)
         turn_back_and_store(*third_half, back_banks[2], nc.scalar)
         combine_on_vector(1, (half, T - P, T), None)

@@ -230,11 +230,10 @@ def tile_moe_rag_mlp_relu_kernel(
             nc.vector.tensor_tensor(product[:], ys[b][:].indirect(entries), gates[:, r, lo:hi], MULT)
             return product
 
-        def turn_and_add(b, lo, hi, k):
-            products = gated(b, 0, lo, hi), gated(b, 1, lo, hi)
+        def turn_and_add(b, lo, hi, first, second, k):
             n = (hi - lo) // P
             turned = bank(k)
-            for r, product in enumerate(products):
+            for r, product in enumerate((first, second)):
                 for c in range(n):
                     nc.tensor.matmul(
                         turned[:, c, :],
@@ -257,34 +256,31 @@ def tile_moe_rag_mlp_relu_kernel(
             nc.scalar.copy(result[:], back[:, 0:n, :])
             queue.dma_start(out=out[b * P : (b + 1) * P, lo:hi], in_=result[:].rearrange("p c t -> p (c t)"))
 
-        def add_and_store(b, first_product, second_product, lo, hi):
+        def add_and_store(b, first, second, lo, hi):
             result = keep.tile([P, hi - lo], F32, name=f"result{b}_{lo}", align_bytes=64)
-            nc.vector.tensor_tensor(result[:], first_product, second_product, ADD)
+            nc.vector.tensor_tensor(result[:], first, second, ADD)
             nc.sync.dma_start(out=out[b * P : (b + 1) * P, lo:hi], in_=result[:])
 
-        def combine_on_vector(b, cuts, waiting):
-            first_product = gated(b, 0, cuts[0], cuts[-1])
+        wide, narrow = 4 * P, 2 * P
+        layer2(2, high, bank_a, nc.scalar.copy)
+        layer2(2, middle, bank_b, nc.scalar.copy)
+        first = gated(0, 0, 0, T)
+        unit1 = turn_and_add(0, 0, wide, first[:, 0:wide], gated(0, 1, 0, wide)[:], bank_c)
+        layer2(2, low, bank_of(1), nc.scalar.copy)
+        unit2 = turn_and_add(0, wide, T, first[:, wide:T], gated(0, 1, wide, T)[:], bank_a)
+        turn_back_and_store(*unit1, bank_of(5), nc.sync)
+        first = gated(1, 0, 0, T)
+        second = gated(1, 1, narrow, T)
+        unit3 = turn_and_add(1, 0, narrow, first[:, 0:narrow], gated(1, 1, 0, narrow)[:], bank_of(1))
+        add_and_store(1, first[:, narrow:T], second[:], narrow, T)
+        turn_back_and_store(*unit2, bank_of(6), nc.scalar)
+        turn_back_and_store(*unit3, bank_of(7), nc.scalar)
+        first = gated(2, 0, 0, T)
+        cuts = (0, narrow, wide, T - P, T)
+        waiting = None
+        for lo, hi in zip(cuts[:-1], cuts[1:]):
+            second = gated(2, 1, lo, hi)
             if waiting is not None:
                 add_and_store(*waiting)
-                waiting = None
-            for lo, hi in zip(cuts[:-1], cuts[1:]):
-                second_product = gated(b, 1, lo, hi)
-                if waiting is not None:
-                    add_and_store(*waiting)
-                waiting = (b, first_product[:, lo - cuts[0] : hi - cuts[0]], second_product[:], lo, hi)
-            add_and_store(*waiting)
-
-        half = T // 2
-        back_banks = [bank_of(c) for c in (7, 6, 5)]
-        layer2(2, high, bank_a, nc.scalar.copy)
-        first_half = turn_and_add(0, 0, half, bank_b)
-        layer2(2, middle, bank_c, nc.scalar.copy)
-        second_half = turn_and_add(0, half, T, bank_a)
-        layer2(2, low, bank_b, nc.scalar.copy)
-        turn_back_and_store(*first_half, back_banks[0], nc.sync)
-        third_half = turn_and_add(1, 0, half, bank_c)
-        turn_back_and_store(*second_half, back_banks[1], nc.scalar)
-        turn_back_and_store(*third_half, back_banks[2], nc.scalar)
-        combine_on_vector(1, (half, T - P, T), None)
-        early = gated(2, 0, 0, half), gated(2, 1, 0, half)
-        combine_on_vector(2, (half, T - P, T), (2, early[0][:], early[1][:], 0, half))
+            waiting = (2, first[:, lo:hi], second[:], lo, hi)
+        add_and_store(*waiting)

@@ -163,7 +163,8 @@ def tile_moe_rag_mlp_relu_kernel(
         def bank_of(c):
             return (CHUNKS - 1 - c) % BANKS
 
-        h_bf16 = {lo: keep.tile([P, (hi - lo) * CH, PACK], BF16, name=f"h_bf16{lo}", align_bytes=64) for lo, hi in groups}
+        h_bf16 = {lo: keep.tile([P, (hi - lo) * CH, PACK], BF16, name=f"h_bf16{lo}", align_bytes=64)[:] for lo, hi in groups[:-1]}
+        h_bf16[0] = ys[0][:, PACK * CH : PACK * CH + 2 * CH].bitcast(BF16).rearrange("p (n t) -> p n t", t=PACK)
         for g, g_end in groups:
             for c in reversed(range(g, g_end)):
                 e = expert[c]
@@ -192,7 +193,7 @@ def tile_moe_rag_mlp_relu_kernel(
             nc.vector.quantize_mx(
                 out=h_codes[g][:].bitcast(FP8X4),
                 scales=h_scales[g][:],
-                in_=h_bf16[g][:].rearrange("p n t -> p (n t)"),
+                in_=h_bf16[g].rearrange("p n t -> p (n t)"),
             )
 
         def layer2(b, chunks, k, copy):
@@ -215,11 +216,11 @@ def tile_moe_rag_mlp_relu_kernel(
             copy(ys[b][:, first * CH : last * CH], flat[:, 0 : (last - first) * CH])
 
         high, middle, low = from_the_end((PACK, PACK, PACK))
-        bank_a, bank_b, bank_c = bank_of(3), bank_of(2), bank_of(0)
-        layer2(0, high, bank_a, nc.scalar.copy)
-        layer2(0, middle, bank_b, nc.scalar.copy)
-        layer2(0, (1, 4), bank_of(1), nc.vector.tensor_copy)
-        layer2(0, (0, 1), bank_of(4), nc.vector.tensor_copy)
+        bank_a, bank_b, bank_c = bank_of(1), bank_of(2), bank_of(0)
+        layer2(0, high, bank_of(3), nc.scalar.copy)
+        layer2(0, middle, bank_b, nc.vector.tensor_copy)
+        layer2(0, (2, 4), bank_a, nc.scalar.copy)
+        layer2(0, (0, 2), bank_c, nc.scalar.copy)
         layer2(1, high, bank_a, nc.scalar.copy)
         layer2(1, middle, bank_b, nc.scalar.copy)
         layer2(1, low, bank_c, nc.scalar.copy)
@@ -266,12 +267,12 @@ def tile_moe_rag_mlp_relu_kernel(
         layer2(2, middle, bank_b, nc.scalar.copy)
         first = gated(0, 0, 0, T)
         unit1 = turn_and_add(0, 0, wide, first[:, 0:wide], gated(0, 1, 0, wide)[:], bank_c)
-        layer2(2, low, bank_of(1), nc.scalar.copy)
-        unit2 = turn_and_add(0, wide, T, first[:, wide:T], gated(0, 1, wide, T)[:], bank_a)
+        layer2(2, low, bank_a, nc.scalar.copy)
+        unit2 = turn_and_add(0, wide, T, first[:, wide:T], gated(0, 1, wide, T)[:], bank_b)
         turn_back_and_store(*unit1, bank_of(5), nc.sync)
         first = gated(1, 0, 0, T)
         second = gated(1, 1, narrow, T)
-        unit3 = turn_and_add(1, 0, narrow, first[:, 0:narrow], gated(1, 1, 0, narrow)[:], bank_of(1))
+        unit3 = turn_and_add(1, 0, narrow, first[:, 0:narrow], gated(1, 1, 0, narrow)[:], bank_a)
         add_and_store(1, first[:, narrow:T], second[:], narrow, T)
         turn_back_and_store(*unit2, bank_of(6), nc.scalar)
         turn_back_and_store(*unit3, bank_of(7), nc.scalar)

@@ -16,7 +16,7 @@ FLOPS = 2 * S * (K * H + H * N)
 
 X_TOKENS = (384, 256, 128)
 X_ON_VECTOR = (192, 112, 80)
-GATHER_CHUNKS = (1, 2, 3, 3, 3)
+GATHER_CHUNKS = (1, 1, 2, 4, 4)
 GROUP_CHUNKS = (4, 4, 2, 1, 1)
 RELU_ON_VECTOR = (4, 2)
 
@@ -147,7 +147,12 @@ def tile_moe_rag_mlp_relu_kernel(
         w1_rest = keep.tile([P, E - 1, 3 * H], U8, name=f"w1_raw{lead}", align_bytes=64)
         for i, e in enumerate(order[1:]):
             w1_codes[e], w1s[e] = w1_rest[:, i, 0 : 2 * H], w1_rest[:, i, 2 * H : 3 * H]
-            permute(nc.gpsimd, w1_codes[e].bitcast(U16), w1_raw[e].bitcast(U16))
+            if i == 0:
+                w1_codes[e] = keep.tile([P, 2 * H], U8, name="w1_second", align_bytes=64)[:]
+                words = w1_codes[e].bitcast(U16).rearrange("p (t m) -> p t m", t=PACK)
+                nc.scalar.copy(words, w1_raw[e].bitcast(U16).rearrange("p (m t) -> p t m", t=PACK))
+            else:
+                permute(nc.gpsimd, w1_codes[e].bitcast(U16), w1_raw[e].bitcast(U16))
             permute(nc.gpsimd, w1s[e], w1s_raw_rest[:, e, :])
 
         slot_words = keep.tile([P, S], U32, name="slot_words", align_bytes=64)
@@ -181,7 +186,10 @@ def tile_moe_rag_mlp_relu_kernel(
                     )
                 dst = h_bf16[g][:, (c - g) * CH : (c - g + 1) * CH, :]
                 src = sums[:].rearrange("p t n -> p n t")
-                if c in RELU_ON_VECTOR:
+                if c == 6:
+                    nc.scalar.activation(dst[:, 0 : CH // 2, :], src[:, 0 : CH // 2, :], RELU)
+                    nc.vector.tensor_scalar_max(dst[:, CH // 2 : CH, :], src[:, CH // 2 : CH, :], 0.0)
+                elif c in RELU_ON_VECTOR:
                     nc.vector.tensor_scalar_max(dst, src, 0.0)
                 else:
                     nc.scalar.activation(dst, src, RELU)

@@ -16,7 +16,7 @@ FLOPS = 2 * S * (K * H + H * N)
 
 X_TOKENS = (384, 256, 128)
 X_ON_VECTOR = (192, 112, 80)
-GATHER_CHUNKS = (1, 1, 2, 4, 4)
+GATHER_CHUNKS = (1, 1, 2, 2, 3, 3)
 GROUP_CHUNKS = (4, 4, 2, 1, 1)
 RELU_ON_VECTOR = (4, 2)
 
@@ -186,10 +186,7 @@ def tile_moe_rag_mlp_relu_kernel(
                     )
                 dst = h_bf16[g][:, (c - g) * CH : (c - g + 1) * CH, :]
                 src = sums[:].rearrange("p t n -> p n t")
-                if c == 6:
-                    nc.scalar.activation(dst[:, 0 : CH // 2, :], src[:, 0 : CH // 2, :], RELU)
-                    nc.vector.tensor_scalar_max(dst[:, CH // 2 : CH, :], src[:, CH // 2 : CH, :], 0.0)
-                elif c in RELU_ON_VECTOR:
+                if c in RELU_ON_VECTOR:
                     nc.vector.tensor_scalar_max(dst, src, 0.0)
                 else:
                     nc.scalar.activation(dst, src, RELU)

from contextlib import ExitStack

import concourse.mybir as mybir
from concourse.masks import make_identity

K, T, E, H, N = 512, 768, 4, 512, 384
COUNTS = (256, 384, 512, 384)
S = sum(COUNTS)
P = 128
PACK = 4
CH = 128
CHUNKS = S // CH
BANKS = 8
LIST = 16
FLOPS = 2 * S * (K * H + H * N)

X_TOKENS = (384, 256, 128)
X_ON_VECTOR = (192, 112, 80)
GATHER_CHUNKS = (1, 1, 2, 2, 3, 3)
GROUP_CHUNKS = (4, 4, 2, 1, 1)
RELU_ON_VECTOR = (4, 2)

F32 = mybir.dt.float32
BF16 = mybir.dt.bfloat16
I32 = mybir.dt.int32
U32 = mybir.dt.uint32
U16 = mybir.dt.uint16
U8 = mybir.dt.uint8
FP8X4 = mybir.dt.float8_e4m3fn_x4
FP4X4 = mybir.dt.float4_e2m1fn_x4
COPY = mybir.ActivationFunctionType.Copy
RELU = mybir.ActivationFunctionType.Relu
MULT = mybir.AluOpType.mult
ADD = mybir.AluOpType.add


def runs(n):
    cut, lo = [], 0
    for width in (512, 256, 128):
        while n - lo >= width:
            cut.append((lo, lo + width))
            lo = lo + width
    return cut


def from_the_end(sizes):
    ranges, hi = [], CHUNKS
    for size in sizes:
        ranges.append((hi - size, hi))
        hi = hi - size
    return ranges


def tile_moe_rag_mlp_relu_kernel(
    tc, xT, w1_words, w1_scales, w2_words, w2_scales, gate, offs, pos1, pos2, out
):
    nc = tc.nc
    order = list(reversed(range(E)))
    lead = order[0]
    x_first = [sum(X_TOKENS[:c]) for c in range(len(X_TOKENS))]
    x_last = len(X_TOKENS) - 1
    expert = [e for e in range(E) for s in range(0, COUNTS[e], CH)]
    groups = from_the_end(GROUP_CHUNKS)

    with ExitStack() as ctx:
        lists = ctx.enter_context(tc.tile_pool(name="lists", bufs=1))
        keep = ctx.enter_context(tc.tile_pool(name="keep", bufs=1))
        psum = ctx.enter_context(tc.psum_pool(name="psum", bufs=1))

        offs_t = lists.tile([P, S // LIST], U16, name="offs_t")
        pos1_t = lists.tile([P, T // LIST], U16, name="pos1_t")
        pos2_t = lists.tile([P, T // LIST], U16, name="pos2_t")

        w1_raw = {e: keep.tile([P, 2 * H], U8, name=f"w1_raw{e}", align_bytes=64)[:] for e in order}
        w1s_raw_lead = keep.tile([P, H], U8, name="w1s_raw_lead", align_bytes=64)[:]
        w1s_raw_rest = keep.tile([P, E - 1, H], U8, name="w1s_raw_rest", align_bytes=64)
        w2_codes = keep.tile([P, E, 2 * N], U8, name="w2_codes", align_bytes=64)
        w2s = keep.tile([P, E, N], U8, name="w2s", align_bytes=64)
        x_raw = [keep.tile([P, PACK, w], F32, name=f"x_raw{c}", align_bytes=64) for c, w in enumerate(X_TOKENS)]
        x_scales = keep.tile([P, T], U8, name="x_scales", align_bytes=64)
        gates = keep.tile([P, 2, T], F32, name="gates", align_bytes=64)
        ident = keep.tile([P, P], F32, name="ident", align_bytes=64)
        ys = [keep.tile([P, S], F32, name=f"y{b}", align_bytes=64) for b in range(N // P)]

        nc.vector.memset(w1s_raw_lead.bitcast(I32), 0)
        nc.vector.memset(w1s_raw_rest[:].rearrange("p e n -> p (e n)").bitcast(I32), 0)
        nc.vector.memset(ident[:], 0.0)
        make_identity(nc, ident[:], nomemset=True)
        nc.vector.memset(x_scales[:].bitcast(I32), 0)
        nc.vector.memset(w2s[:].rearrange("p e n -> p (e n)").bitcast(I32), 0)

        def load_w1_words(e):
            nc.sync.dma_start(out=w1_raw[e].bitcast(I32), in_=w1_words[e, 0].bitcast(I32))

        def load_scale_rows(tile, rows):
            for q in range(4):
                nc.sync.dma_start(out=tile[32 * q : 32 * q + 4].bitcast(I32), in_=rows[4 * q : 4 * q + 4].bitcast(I32))

        by_word = xT.rearrange("(p j) w -> p j w", j=PACK)
        nc.sync.dma_start(out=x_raw[0][:], in_=by_word[:, :, 0 : X_TOKENS[0]])
        load_scale_rows(w1s_raw_lead, w1_scales[lead, 0])
        for c in range(1, len(X_TOKENS)):
            nc.sync.dma_start(out=x_raw[c][:], in_=by_word[:, :, x_first[c] : x_first[c] + X_TOKENS[c]])
        load_w1_words(lead)
        nc.sync.dma_start(offs_t[:], offs)
        load_w1_words(order[1])
        load_scale_rows(w1s_raw_rest, w1_scales[0:lead, 0].rearrange("e q n -> q e n"))
        load_w1_words(order[2])
        load_w1_words(order[3])
        nc.sync.dma_start(out=w2_codes[:].bitcast(I32), in_=w2_words[:, 0].rearrange("e p b -> p e b").bitcast(I32))
        load_scale_rows(w2s, w2_scales[:, 0].rearrange("e q n -> q e n"))
        nc.sync.dma_start(pos1_t[:], pos1)
        nc.sync.dma_start(pos2_t[:], pos2)
        nc.sync.dma_start(out=gates[:], in_=gate[:, 0:P, :].rearrange("g p t -> p g t"))

        x_codes = keep.tile([P, T], U32, name="x_codes", align_bytes=64)
        x_bf16 = [keep.tile([P, w, PACK], BF16, name=f"x_bf16{c}", align_bytes=64) for c, w in enumerate(X_TOKENS)]

        def quantise_tokens(c):
            for lo, hi in ((0, CH), (CH, X_TOKENS[c])) if c == 0 else runs(X_TOKENS[c]):
                nc.vector.quantize_mx(
                    out=x_codes[:, x_first[c] + lo : x_first[c] + hi].bitcast(FP8X4),
                    scales=x_scales[:, x_first[c] + lo : x_first[c] + hi],
                    in_=x_bf16[c][:, lo:hi, :].rearrange("p w j -> p (w j)"),
                )

        def interleaving(c, lo, hi):
            dst = x_bf16[c][:, lo:hi, :].rearrange("p (c i) t -> p c t i", i=4)
            src = x_raw[c][:, :, lo:hi].rearrange("p t (c i) -> p c t i", i=4)
            return dst, src

        def permute(engine, dst, src):
            engine.tensor_copy(dst.rearrange("p (t m) -> p t m", t=PACK), src.rearrange("p (m t) -> p t m", t=PACK))

        w1s = {lead: keep.tile([P, H], U8, name="w1s_lead", align_bytes=64)[:]}
        for c, w in enumerate(X_TOKENS):
            nc.vector.tensor_copy(*interleaving(c, 0, X_ON_VECTOR[c]))
            nc.scalar.activation(*interleaving(c, X_ON_VECTOR[c], w), COPY)
            if c == 0:
                permute(nc.vector, w1s[lead], w1s_raw_lead)
            else:
                quantise_tokens(c - 1)
        quantise_tokens(x_last)

        w1_codes = {lead: keep.tile([P, 2 * H], U8, name=f"x_raw{x_last}", align_bytes=64)[:]}
        permute(nc.vector, w1_codes[lead].bitcast(U16), w1_raw[lead].bitcast(U16))
        w1_rest = keep.tile([P, E - 1, 3 * H], U8, name=f"w1_raw{lead}", align_bytes=64)
        for i, e in enumerate(order[1:]):
            w1_codes[e], w1s[e] = w1_rest[:, i, 0 : 2 * H], w1_rest[:, i, 2 * H : 3 * H]
            if i == 0:
                w1_codes[e] = keep.tile([P, 2 * H], U8, name="w1_second", align_bytes=64)[:]
                words = w1_codes[e].bitcast(U16).rearrange("p (t m) -> p t m", t=PACK)
                nc.scalar.copy(words, w1_raw[e].bitcast(U16).rearrange("p (m t) -> p t m", t=PACK))
            else:
                permute(nc.gpsimd, w1_codes[e].bitcast(U16), w1_raw[e].bitcast(U16))
            permute(nc.gpsimd, w1s[e], w1s_raw_rest[:, e, :])

        slot_words = keep.tile([P, S], U32, name="slot_words", align_bytes=64)
        slot_bytes = keep.tile([P, S], U8, name="slot_bytes", align_bytes=64)
        for lo, hi in from_the_end(GATHER_CHUNKS):
            entries = offs_t[:, lo * CH // LIST : hi * CH // LIST]
            nc.vector.tensor_copy(slot_words[:, lo * CH : hi * CH], x_codes[:].indirect(entries))
            nc.vector.tensor_copy(slot_bytes[:, lo * CH : hi * CH], x_scales[:].indirect(entries))

        def bank(k):
            return psum.tile([P, PACK, CH], F32, name=f"bank{k}", bufs=1)

        def bank_of(c):
            return (CHUNKS - 1 - c) % BANKS

        h_bf16 = {lo: keep.tile([P, (hi - lo) * CH, PACK], BF16, name=f"h_bf16{lo}", align_bytes=64)[:] for lo, hi in groups[:-1]}
        h_bf16[0] = ys[0][:, PACK * CH : PACK * CH + 2 * CH].bitcast(BF16).rearrange("p (n t) -> p n t", t=PACK)
        for g, g_end in groups:
            for c in reversed(range(g, g_end)):
                e = expert[c]
                sums = bank(bank_of(c))
                for t in range(PACK):
                    nc.tensor.matmul_mx(
                        out=sums[:, t, :],
                        lhsT=w1_codes[e][:, 2 * P * t : 2 * P * (t + 1)].bitcast(FP4X4),
                        lhsT_scale=w1s[e][:, P * t : P * (t + 1)],
                        rhs=slot_words[:, c * CH : (c + 1) * CH].bitcast(FP8X4),
                        rhs_scale=slot_bytes[:, c * CH : (c + 1) * CH],
                        start=True,
                        stop=True,
                    )
                dst = h_bf16[g][:, (c - g) * CH : (c - g + 1) * CH, :]
                src = sums[:].rearrange("p t n -> p n t")
                if c in RELU_ON_VECTOR:
                    nc.vector.tensor_scalar_max(dst, src, 0.0)
                else:
                    nc.scalar.activation(dst, src, RELU)

        h_codes, h_scales = {}, {}
        for g, g_end in groups:
            h_codes[g] = keep.tile([P, (g_end - g) * CH], U32, name=f"h_codes{g}", align_bytes=64)
            h_scales[g] = keep.tile([P, (g_end - g) * CH], U8, name=f"h_scales{g}", align_bytes=64)
            nc.vector.quantize_mx(
                out=h_codes[g][:].bitcast(FP8X4),
                scales=h_scales[g][:],
                in_=h_bf16[g].rearrange("p n t -> p (n t)"),
            )

        def layer2(b, chunks, k, copy):
            first, last = chunks
            flat = bank(k)[:].rearrange("p t n -> p (t n)")
            for g, g_end in groups:
                for e in order:
                    mine = [c for c in range(max(first, g), min(last, g_end)) if expert[c] == e]
                    for lo, hi in runs(len(mine) * CH):
                        in_group = slice((mine[0] - g) * CH + lo, (mine[0] - g) * CH + hi)
                        nc.tensor.matmul_mx(
                            out=flat[:, (mine[0] - first) * CH + lo : (mine[0] - first) * CH + hi],
                            lhsT=w2_codes[:, e, 2 * P * b : 2 * P * (b + 1)].bitcast(FP4X4),
                            lhsT_scale=w2s[:, e, P * b : P * (b + 1)],
                            rhs=h_codes[g][:, in_group].bitcast(FP8X4),
                            rhs_scale=h_scales[g][:, in_group],
                            start=True,
                            stop=True,
                        )
            copy(ys[b][:, first * CH : last * CH], flat[:, 0 : (last - first) * CH])

        high, middle, low = from_the_end((PACK, PACK, PACK))
        bank_a, bank_b, bank_c = bank_of(1), bank_of(2), bank_of(0)
        layer2(0, high, bank_of(3), nc.scalar.copy)
        layer2(0, middle, bank_b, nc.vector.tensor_copy)
        layer2(0, (2, 4), bank_a, nc.scalar.copy)
        layer2(0, (0, 2), bank_c, nc.scalar.copy)
        layer2(1, high, bank_a, nc.scalar.copy)
        layer2(1, middle, bank_b, nc.scalar.copy)
        layer2(1, low, bank_c, nc.scalar.copy)

        def gated(b, r, lo, hi):
            product = keep.tile([P, hi - lo], F32, name=f"product{b}_{r}_{lo}", align_bytes=64)
            entries = (pos1_t, pos2_t)[r][:, lo // LIST : hi // LIST]
            nc.vector.tensor_tensor(product[:], ys[b][:].indirect(entries), gates[:, r, lo:hi], MULT)
            return product

        def turn_and_add(b, lo, hi, first, second, k):
            n = (hi - lo) // P
            turned = bank(k)
            for r, product in enumerate((first, second)):
                for c in range(n):
                    nc.tensor.matmul(
                        turned[:, c, :],
                        product[:, c * P : (c + 1) * P],
                        ident[:],
                        start=(r, c) == (0, 0),
                        stop=(r, c) == (1, n - 1),
                        is_transpose=True,
                    )
            total = keep.tile([P, n, P], F32, name=f"turned{b}_{lo}", align_bytes=64)
            nc.scalar.copy(total[:], turned[:, 0:n, :])
            return b, lo, hi, total

        def turn_back_and_store(b, lo, hi, total, k, queue):
            n = (hi - lo) // P
            back = bank(k)
            for c in range(n):
                nc.tensor.transpose(back[:, c, :], total[:, c, :], ident[:])
            result = keep.tile([P, n, P], F32, name=f"result{b}_{lo}", align_bytes=64)
            nc.scalar.copy(result[:], back[:, 0:n, :])
            queue.dma_start(out=out[b * P : (b + 1) * P, lo:hi], in_=result[:].rearrange("p c t -> p (c t)"))

        def add_and_store(b, first, second, lo, hi):
            result = keep.tile([P, hi - lo], F32, name=f"result{b}_{lo}", align_bytes=64)
            nc.vector.tensor_tensor(result[:], first, second, ADD)
            nc.sync.dma_start(out=out[b * P : (b + 1) * P, lo:hi], in_=result[:])

        wide, narrow = 4 * P, 2 * P
        layer2(2, high, bank_a, nc.scalar.copy)
        layer2(2, middle, bank_b, nc.scalar.copy)
        first = gated(0, 0, 0, T)
        unit1 = turn_and_add(0, 0, wide, first[:, 0:wide], gated(0, 1, 0, wide)[:], bank_c)
        layer2(2, low, bank_a, nc.scalar.copy)
        unit2 = turn_and_add(0, wide, T, first[:, wide:T], gated(0, 1, wide, T)[:], bank_b)
        turn_back_and_store(*unit1, bank_of(5), nc.sync)
        first = gated(1, 0, 0, T)
        second = gated(1, 1, narrow, T)
        unit3 = turn_and_add(1, 0, narrow, first[:, 0:narrow], gated(1, 1, 0, narrow)[:], bank_a)
        add_and_store(1, first[:, narrow:T], second[:], narrow, T)
        turn_back_and_store(*unit2, bank_of(6), nc.scalar)
        turn_back_and_store(*unit3, bank_of(7), nc.scalar)
        first = gated(2, 0, 0, T)
        cuts = (0, narrow, wide, T - P, T)
        waiting = None
        for lo, hi in zip(cuts[:-1], cuts[1:]):
            second = gated(2, 1, lo, hi)
            if waiting is not None:
                add_and_store(*waiting)
            waiting = (2, first[:, lo:hi], second[:], lo, hi)
        add_and_store(*waiting)
